import numpy as np
import ml_dtypes


def mxq(x, axis, fmt="e4m3"):
    dtype, down = {"e4m3": (ml_dtypes.float8_e4m3fn, 7), "e5m2": (ml_dtypes.float8_e5m2, 14)}[fmt]
    v = np.moveaxis(np.asarray(x, np.float32).astype(ml_dtypes.bfloat16).astype(np.float64), axis, -1)
    blocks = v.reshape(v.shape[:-1] + (-1, 32))
    amax = np.abs(blocks).max(-1, keepdims=True)
    byte = np.maximum(np.where(amax > 0, np.frexp(amax)[1] - 1 + 127, 0) - down, 1)
    scale = np.exp2(byte - 127.0)
    codes = (blocks / scale).astype(np.float32).astype(dtype).astype(np.float64)
    return np.moveaxis((codes * scale).reshape(v.shape), -1, axis)


WIDE = False


def mx_kscale(k):
    if not WIDE:
        return np.ones(k)
    levels = np.array([10, -10, 5, -5, 0])
    if k % 512:
        return np.exp2(np.random.permutation(np.resize(levels, k // 32))).repeat(32)
    a = np.empty((k // 512, 16))
    for p in range(k // 512):
        a[p, :8] = np.random.permutation(np.resize(levels, 8))
        for g in range(8):
            far = levels[np.abs(levels - a[p, g]) >= 10]
            a[p, g + 8] = far[np.random.randint(len(far))]
    return np.exp2(a.ravel()).repeat(32)


def f64(x):
    return np.asarray(x).astype(np.float64)


def striped(idx):
    return np.tile(idx.reshape(-1, 16).T, (8, 1)).astype(np.uint16)


def unstriped(offs):
    return offs[:16].T.reshape(-1).astype(np.int64)


E2M1 = np.array([0.0, 0.5, 1.0, 1.5, 2.0, 3.0, 4.0, 6.0, -0.0, -0.5, -1.0, -1.5, -2.0, -3.0, -4.0, -6.0])


def pack_weight(w, fmt):
    k, n = w.shape
    w = f64(np.asarray(w, np.float32).astype(ml_dtypes.bfloat16)).reshape(k // 32, 32, n)
    amax = np.abs(w).max(1)
    if fmt == "e4m3":
        byte = np.frexp(amax)[1] - 1 + 127 - 7
    else:
        mant, ex = np.frexp(amax / 6.0)
        byte = np.where(mant > 0.5, ex, ex - 1) + 127
    byte = np.clip(np.where(amax > 0, byte, 1), 1, 254)
    scaled = (w * np.exp2(127.0 - byte)[:, None, :]).reshape(k, n).astype(np.float32)
    by_word = np.ascontiguousarray(scaled.reshape(k // 512, 128, 4, n).transpose(0, 1, 3, 2))
    if fmt == "e4m3":
        words = by_word.astype(ml_dtypes.float8_e4m3fn).view(np.uint8)
    else:
        c = by_word.astype(ml_dtypes.float4_e2m1fn).view(np.uint8) & 0xF
        words = (c[..., 0::2] | (c[..., 1::2] << 4)).reshape(k // 512, 128, 2 * n)
    return np.ascontiguousarray(words), np.ascontiguousarray(byte.astype(np.uint8).reshape(k // 512, 16, n))


def unpack_weight(words, scales, fmt):
    g, _, n = scales.shape
    words = np.ascontiguousarray(words).reshape(g, 128, n, -1)
    if fmt == "e4m3":
        vals = words.view(ml_dtypes.float8_e4m3fn).astype(np.float64)
    else:
        nib = np.empty((g, 128, n, 4), np.uint8)
        nib[..., 0::2] = words & 0xF
        nib[..., 1::2] = words >> 4
        vals = E2M1[nib]
    vals = vals * np.repeat(np.exp2(scales.astype(np.float64) - 127.0), 8, axis=1)[..., None]
    return vals.transpose(0, 1, 3, 2).reshape(g * 512, n)


def gelu(v):
    return 0.5 * v * (1.0 + np.tanh(np.sqrt(2.0 / np.pi) * (v + 0.044715 * v**3)))


K, H, N, T, S, T2, P = 1536, 1024, 512, 2048, 1024, 2048, 512


def setup_inputs():
    n = np.random.standard_normal
    s = mx_kscale(K)[:, None]
    u = mx_kscale(H)[:, None]
    tab_words, tab_scales = pack_weight(n((K, T)) * s, "e4m3")
    w2_words, w2_scales = pack_weight(n((H, N)) / u / np.sqrt(H), "e2m1")
    return {
        "tab_words": tab_words, "tab_scales": tab_scales,
        "offs": striped(np.random.permutation(T)[:S]),
        "offs2": striped(np.random.permutation(T2)[:S]),
        "offs3": striped(np.random.permutation(T2)[:P]),
        "w1": (0.7 * n((K, H)) / s / np.sqrt(K)).astype(np.float32),
        "wgs": np.exp(0.3 * n((128, S))).astype(np.float32),
        "page0": (0.8 * n((H, T2))).astype(np.float32),
        "fam": (8.0 * n((H, P)) * u).astype(np.float32),
        "w2_words": w2_words, "w2_scales": w2_scales,
        "w3": (n((H, N)) / u / np.sqrt(H)).astype(np.float32),
        "base": (0.6 * n(N)).astype(np.float32),
    }


def reference(tab_words, tab_scales, offs, offs2, offs3, w1, wgs, page0, fam,
              w2_words, w2_scales, w3, base):
    v = unpack_weight(tab_words, tab_scales, "e4m3")[:, unstriped(offs)]
    h = mxq(f64(w1), 0, "e4m3").T @ v
    page = f64(page0).copy()
    page[:, unstriped(offs2)] = np.tile(f64(wgs), (H // 128, 1)) * h
    top = page.max(axis=1)
    a = np.exp(page[:, unstriped(offs3)] - top[:, None])
    q = mxq(a * f64(fam), 0, "e4m3")
    y = unpack_weight(w2_words, w2_scales, "e2m1").T @ q
    d = mxq(f64(w3), 0, "e4m3").T @ q
    return np.maximum(y, d + f64(base)[:, None])

@@ -1,0 +1,321 @@
+from contextlib import ExitStack
+
+import concourse.mybir as mybir
+
+K, H, N, T, S, T2, M = 1536, 1024, 512, 2048, 1024, 2048, 512
+FLOPS = 2 * K * H * S + 2 * 2 * H * N * M
+
+F32 = mybir.dt.float32
+BF16 = mybir.dt.bfloat16
+I32 = mybir.dt.int32
+U32 = mybir.dt.uint32
+U16 = mybir.dt.uint16
+U8 = mybir.dt.uint8
+FP8X4 = mybir.dt.float8_e4m3fn_x4
+FP4X4 = mybir.dt.float4_e2m1fn_x4
+ALU = mybir.AluOpType
+ACT = mybir.ActivationFunctionType
+AXIS = mybir.AxisListType
+
+P = 128
+PACK = 4
+PASS = P * PACK
+K_PASSES = K // PASS
+R_PASSES = H // PASS
+TILES = R_PASSES * PACK
+BANK = 512
+QUAD = 32
+H_SLOTS = 4
+
+
+def tile_list_register_reread_features_kernel(
+    tc, tab_words, tab_scales, offs, offs2, offs3, w1, wgs, page0, fam, w2_words, w2_scales, w3, base, out
+):
+    nc = tc.nc
+    with ExitStack() as ctx:
+        lists = ctx.enter_context(tc.tile_pool(name="lists", bufs=1))
+        keep = ctx.enter_context(tc.tile_pool(name="keep", bufs=1))
+        ring = ctx.enter_context(tc.tile_pool(name="ring", bufs=1))
+        psum = ctx.enter_context(tc.psum_pool(name="psum", bufs=8))
+
+        idx = lists.tile([P, S // 16], U16, name="idx")
+        idx2 = lists.tile([P, S // 16], U16, name="idx2")
+        idx3 = lists.tile([P, M // 16], U16, name="idx3")
+
+        tab_plane = keep.tile([P, T], U8, name="tab_plane", align_bytes=64)
+        w2_plane = keep.tile([P, R_PASSES, N], U8, name="w2_plane", align_bytes=64)
+        w2_codes = keep.tile([P, R_PASSES, 2 * N], U8, name="w2_codes", align_bytes=64)
+        base_sb = keep.tile([P, N // P], F32, name="base_sb")
+        neg_top = [keep.tile([P, 1], F32, name="neg_top%d" % i) for i in range(TILES)]
+        wgs_sb = [keep.tile([P, S], F32, name="wgs%d" % t) for t in range(PACK)]
+        fam_sb = [keep.tile([P, PACK, M], F32, name="fam%d" % b) for b in range(R_PASSES)]
+
+        nc.vector.memset(tab_plane[:].bitcast(I32), 0)
+        nc.gpsimd.memset(w2_plane[:].rearrange("p a n -> p (a n)").bitcast(I32), 0)
+
+        tab_sb, w1_raw, w3_raw, page = {}, {}, {}, {}
+
+        def load_tab(a):
+            tab_sb[a] = ring.tile([P, T], I32, name="tab%d" % a, tag="wide", bufs=7)
+            nc.sync.dma_start(out=tab_sb[a][:], in_=tab_words[a].rearrange("p t i -> p (t i)").bitcast(I32))
+
+        def load_w1(a, b):
+            w1_raw[a, b] = ring.tile([P, PACK, PASS], F32, name="w1raw%d%d" % (a, b), tag="raw", bufs=4)
+            rows = w1[a * PASS : (a + 1) * PASS, b * PASS : (b + 1) * PASS]
+            nc.sync.dma_start(out=w1_raw[a, b][:], in_=rows.rearrange("(p j) c -> p j c", j=PACK))
+
+        def load_w3(b):
+            w3_raw[b] = ring.tile([P, PACK, N], F32, name="w3raw%d" % b, tag="raw", bufs=4)
+            nc.sync.dma_start(out=w3_raw[b][:], in_=w3[b * PASS : (b + 1) * PASS, :].rearrange("(p j) n -> p j n", j=PACK))
+
+        def load_wgs(t):
+            for q in range(P // QUAD):
+                nc.sync.dma_start(
+                    out=wgs_sb[t][q * QUAD : (q + 1) * QUAD, :], in_=wgs.rearrange("(g t) j -> t g j", t=PACK)[t]
+                )
+
+        def load_page(i):
+            b, t = divmod(i, PACK)
+            page[i] = ring.tile([P, T2], F32, name="page%d" % i, tag="wide", bufs=7)
+            rows = page0[b * PASS : (b + 1) * PASS, :].rearrange("(p t) c -> t p c", t=PACK)[t]
+            nc.sync.dma_start(out=page[i][:], in_=rows)
+
+        def load_fam(b):
+            nc.sync.dma_start(out=fam_sb[b][:], in_=fam[b * PASS : (b + 1) * PASS, :].rearrange("(p t) m -> p t m", t=PACK))
+
+        nc.sync.dma_start(idx[:], offs)
+        load_tab(0)
+        load_w1(0, 0)
+        scale_rows = keep.tile([P, T // 4], I32, name="scale_rows")
+        for q in range(P // QUAD):
+            live = slice(q * QUAD, q * QUAD + PACK * K_PASSES)
+            nc.sync.dma_start(out=scale_rows[live, :], in_=tab_scales[:, PACK * q : PACK * (q + 1), :].bitcast(I32))
+        for a in range(1, K_PASSES):
+            load_tab(a)
+            load_w1(a, 0)
+        nc.sync.dma_start(idx2[:], offs2)
+        load_wgs(0)
+        load_page(0)
+        load_w1(0, 1)
+        load_w1(1, 1)
+        nc.sync.dma_start(idx3[:], offs3)
+        load_wgs(1)
+        load_page(1)
+        load_w1(2, 1)
+        load_wgs(2)
+        load_page(2)
+        load_fam(0)
+        load_wgs(3)
+        load_page(3)
+        load_page(4)
+        load_w3(0)
+        load_fam(1)
+        load_page(5)
+        load_w3(1)
+        nc.sync.dma_start(out=w2_codes[:].bitcast(I32), in_=w2_words.rearrange("a p c -> p a c").bitcast(I32))
+        for q in range(P // QUAD):
+            nc.sync.dma_start(
+                out=w2_plane[q * QUAD : q * QUAD + PACK, :, :].bitcast(I32),
+                in_=w2_scales[:, PACK * q : PACK * (q + 1), :].rearrange("a r n -> r a n").bitcast(I32),
+            )
+        with nc.allow_non_contiguous_dma(reason="one base value a partition"):
+            nc.sync.dma_start(out=base_sb[:], in_=base.rearrange("(c p) -> p c", p=P))
+        load_page(6)
+        load_page(7)
+
+        v_plane = keep.tile([P, S], U8, name="v_plane", align_bytes=64)
+        v_codes = [keep.tile([P, S], U32, name="v_codes%d" % a, align_bytes=64) for a in range(K_PASSES)]
+        w1_codes, w1_plane, w1_bf = {}, {}, {}
+
+        def gather_words(a, pieces):
+            n = S // pieces
+            for s in range(pieces):
+                nc.vector.tensor_copy(
+                    out=v_codes[a][:, s * n : (s + 1) * n],
+                    in_=tab_sb[a][:].bitcast(U32).indirect(idx[:, s * n // 16 : (s + 1) * n // 16]),
+                )
+
+        def weave_w1(a, b):
+            w1_bf[a, b] = ring.tile([P, PACK, P, PACK], BF16, name="w1bf%d%d" % (a, b), tag="bf", bufs=3, align_bytes=64)
+            nc.scalar.copy(
+                out=w1_bf[a, b][:].rearrange("p t m j -> p m j t"),
+                in_=w1_raw[a, b][:].rearrange("p j (m t) -> p m j t", t=PACK),
+            )
+
+        def quant_w1(a, b):
+            w1_codes[a, b] = keep.tile([P, PASS], U32, name="w1c%d%d" % (a, b), align_bytes=64)
+            w1_plane[a, b] = keep.tile([P, PASS], U8, name="w1s%d%d" % (a, b), align_bytes=64)
+            nc.vector.quantize_mx(
+                out=w1_codes[a, b][:].bitcast(FP8X4),
+                scales=w1_plane[a, b][:],
+                in_=w1_bf[a, b][:].rearrange("p t m j -> p (t m j)"),
+            )
+
+        gather_words(0, 1)
+        for q in range(P // QUAD):
+            live = slice(q * QUAD, q * QUAD + PACK * K_PASSES)
+            nc.vector.tensor_copy(out=tab_plane[live, :].bitcast(I32), in_=scale_rows[live, :])
+        nc.vector.tensor_copy(out=v_plane[:], in_=tab_plane[:].indirect(idx[:]))
+        weave_w1(0, 0)
+        gather_words(1, 1)
+        quant_w1(0, 0)
+        weave_w1(1, 0)
+        gather_words(2, 1)
+        quant_w1(1, 0)
+
+        last = K_PASSES - 1
+        bf_first = keep.tile([P, P, PACK], BF16, name="bf_first", align_bytes=64)
+        bf_rest = ring.tile([P, PACK - 1, P, PACK], BF16, name="bf_rest", tag="bf", bufs=3, align_bytes=64)
+        raw_last = w1_raw[last, 0][:].rearrange("p j (m t) -> p m j t", t=PACK)
+        w1_codes[last, 0] = keep.tile([P, PASS], U32, name="w1c_last", align_bytes=64)
+        w1_plane[last, 0] = keep.tile([P, PASS], U8, name="w1s_last", align_bytes=64)
+        nc.vector.tensor_copy(out=bf_first[:], in_=raw_last[:, :, :, 0])
+        nc.scalar.copy(out=bf_rest[:].rearrange("p t m j -> p m j t"), in_=raw_last[:, :, :, 1:PACK])
+        nc.vector.quantize_mx(
+            out=w1_codes[last, 0][:, 0:P].bitcast(FP8X4),
+            scales=w1_plane[last, 0][:, 0:P],
+            in_=bf_first[:].rearrange("p m j -> p (m j)"),
+        )
+        nc.vector.quantize_mx(
+            out=w1_codes[last, 0][:, P:PASS].bitcast(FP8X4),
+            scales=w1_plane[last, 0][:, P:PASS],
+            in_=bf_rest[:].rearrange("p t m j -> p (t m j)"),
+        )
+
+        h_sb = {}
+
+        def make_h(i):
+            b, t = divmod(i, PACK)
+            h_sb[i] = ring.tile([P, S], F32, name="h%d" % i, tag="h%d" % (i % H_SLOTS), align_bytes=64)
+            cols = slice(t * P, (t + 1) * P)
+            for s in range(S // BANK):
+                part = slice(s * BANK, (s + 1) * BANK)
+                acc = psum.tile([P, BANK], F32, name="hacc%d%d" % (i, s), tag="bank")
+                for a in range(K_PASSES):
+                    nc.tensor.matmul_mx(
+                        out=acc[:],
+                        lhsT=w1_codes[a, b][:, cols].bitcast(FP8X4),
+                        lhsT_scale=w1_plane[a, b][:, cols],
+                        rhs=v_codes[a][:, part].bitcast(FP8X4),
+                        rhs_scale=v_plane[PACK * a : P, part],
+                        start=(a == 0),
+                        stop=(a == K_PASSES - 1),
+                    )
+                nc.scalar.copy(out=h_sb[i][:, part], in_=acc[:])
+
+        x_rows = [keep.tile([P, PACK, M], BF16, name="x_rows0"), keep.tile([P, 2, M], BF16, name="x_rows1")]
+        x_bf = [keep.tile([P, M, PACK], BF16, name="x_bf%d" % b, align_bytes=64) for b in range(R_PASSES)]
+        look_last = keep.tile([P, 2, M], F32, name="look_last")
+
+        def change_page(i):
+            nc.vector.tensor_tensor(
+                out=page[i][:].indirect(idx2[:]), in0=h_sb[i][:], in1=wgs_sb[i % PACK][:], op=ALU.mult
+            )
+            nc.vector.tensor_reduce(out=neg_top[i][:], in_=page[i][:], axis=AXIS.X, op=ALU.max, negate=True)
+
+        def look(i):
+            b, t = divmod(i, PACK)
+            if i >= TILES - 2:
+                looked = look_last[:, t - 2, :]
+            else:
+                looked_tile = ring.tile([P, M], F32, name="look%d" % i, tag="look", bufs=3)
+                looked = looked_tile[:]
+            nc.scalar.activation(out=looked, in_=page[i][:].indirect(idx3[:]), func=ACT.Exp, bias=neg_top[i][:])
+            if i < TILES - 2:
+                nc.gpsimd.tensor_tensor(out=x_rows[b][:, t, :], in0=looked, in1=fam_sb[b][:, t, :], op=ALU.mult)
+
+        w3_bf = {}
+
+        def weave_w3(b):
+            w3_bf[b] = ring.tile([P, N, PACK], BF16, name="w3bf%d" % b, tag="bf", bufs=3, align_bytes=64)
+            nc.scalar.copy(
+                out=w3_bf[b][:].rearrange("p (c i) j -> p c j i", i=PACK),
+                in_=w3_raw[b][:].rearrange("p j (c i) -> p c j i", i=PACK),
+            )
+
+        def quantize(codes, plane, src):
+            nc.vector.quantize_mx(out=codes.bitcast(FP8X4), scales=plane, in_=src.rearrange("p c j -> p (c j)"))
+
+        for i in range(PACK):
+            make_h(i)
+        for a in range(K_PASSES):
+            weave_w1(a, 1)
+        change_page(0)
+        quant_w1(0, 1)
+        look(0)
+        change_page(1)
+        quant_w1(1, 1)
+        quant_w1(2, 1)
+        make_h(4)
+        make_h(5)
+        look(1)
+        change_page(2)
+        make_h(6)
+        look(2)
+        change_page(3)
+        make_h(7)
+        look(3)
+        weave_w3(0)
+        change_page(4)
+        look(4)
+        weave_w3(1)
+        nc.scalar.copy(
+            out=x_bf[0][:].rearrange("p (c i) t -> p c t i", i=PACK),
+            in_=x_rows[0][:].rearrange("p t (c i) -> p c t i", i=PACK),
+        )
+        change_page(5)
+        look(5)
+        w3_plane = [keep.tile([P, N], U8, name="w3s%d" % b, align_bytes=64) for b in range(R_PASSES)]
+        x_plane = [keep.tile([P, M], U8, name="xs%d" % b, align_bytes=64) for b in range(R_PASSES)]
+        w3_first = ring.tile([P, N], U32, name="w3c0", tag="h1", align_bytes=64)
+        quantize(w3_first[:], w3_plane[0][:], w3_bf[0][:])
+        change_page(6)
+        look(6)
+        nc.scalar.copy(out=x_bf[1][:, :, 0:2], in_=x_rows[1][:].rearrange("p t m -> p m t"))
+        change_page(7)
+        look(7)
+        late = ring.tile([P, 2, M], U32, name="late", tag="h3", align_bytes=64)
+        x_last = keep.tile([P, M], U32, name="x_last", align_bytes=64)
+        x_codes = [late[:, 0, :], x_last[:]]
+        w3_codes = [w3_first[:], late[:, 1, :]]
+        quantize(x_codes[0], x_plane[0][:], x_bf[0][:])
+        quantize(w3_codes[1], w3_plane[1][:], w3_bf[1][:])
+        nc.vector.tensor_tensor(
+            out=x_bf[1][:, :, 2:4],
+            in0=look_last[:].rearrange("p t m -> p m t"),
+            in1=fam_sb[1][:, 2:4, :].rearrange("p t m -> p m t"),
+            op=ALU.mult,
+        )
+        quantize(x_codes[1], x_plane[1][:], x_bf[1][:])
+
+        y_acc = [psum.tile([P, BANK], F32, name="y%d" % c, tag="bank") for c in range(N // P)]
+        d_acc = [psum.tile([P, BANK], F32, name="d%d" % c, tag="bank") for c in range(N // P)]
+        for b in range(R_PASSES):
+            for c in range(N // P):
+                cols = slice(c * P, (c + 1) * P)
+                nc.tensor.matmul_mx(
+                    out=y_acc[c][:],
+                    lhsT=w2_codes[:, b, 2 * c * P : 2 * (c + 1) * P].bitcast(FP4X4),
+                    lhsT_scale=w2_plane[:, b, cols],
+                    rhs=x_codes[b].bitcast(FP8X4),
+                    rhs_scale=x_plane[b][:],
+                    start=(b == 0),
+                    stop=(b == R_PASSES - 1),
+                )
+                nc.tensor.matmul_mx(
+                    out=d_acc[c][:],
+                    lhsT=w3_codes[b][:, cols].bitcast(FP8X4),
+                    lhsT_scale=w3_plane[b][:, cols],
+                    rhs=x_codes[b].bitcast(FP8X4),
+                    rhs_scale=x_plane[b][:],
+                    start=(b == 0),
+                    stop=(b == R_PASSES - 1),
+                )
+        for c in range(N // P):
+            y_sb = ring.tile([P, M], F32, name="ysb%d" % c, tag="look", bufs=3)
+            res = ring.tile([P, M], F32, name="res%d" % c, tag="res", bufs=4)
+            nc.scalar.copy(out=y_sb[:], in_=y_acc[c][:])
+            nc.vector.scalar_tensor_tensor(
+                out=res[:], in0=d_acc[c][:], scalar=base_sb[:, c : c + 1], in1=y_sb[:], op0=ALU.add, op1=ALU.max
+            )
+            nc.sync.dma_start(out=out[c * P : (c + 1) * P, :], in_=res[:])

@@ -47,11 +47,12 @@ def tile_list_register_reread_features_kernel(
         w2_codes = keep.tile([P, R_PASSES, 2 * N], U8, name="w2_codes", align_bytes=64)
         base_sb = keep.tile([P, N // P], F32, name="base_sb")
         neg_top = [keep.tile([P, 1], F32, name="neg_top%d" % i) for i in range(TILES)]
-        wgs_sb = [keep.tile([P, S], F32, name="wgs%d" % t) for t in range(PACK)]
+        wgs_nat = keep.tile([P, S], F32, name="wgs_nat")
+        wgs_sb = [ring.tile([P, S], F32, name="wgs%d" % t, tag="wgs%d" % t, align_bytes=64) for t in range(PACK)]
         fam_sb = [keep.tile([P, PACK, M], F32, name="fam%d" % b) for b in range(R_PASSES)]
 
         nc.vector.memset(tab_plane[:].bitcast(I32), 0)
-        nc.gpsimd.memset(w2_plane[:].rearrange("p a n -> p (a n)").bitcast(I32), 0)
+        nc.vector.memset(w2_plane[:].rearrange("p a n -> p (a n)").bitcast(I32), 0)
 
         tab_sb, w1_raw, w3_raw, page = {}, {}, {}, {}
 
@@ -59,13 +60,21 @@ def tile_list_register_reread_features_kernel(
             tab_sb[a] = ring.tile([P, T], I32, name="tab%d" % a, tag="wide", bufs=7)
             nc.sync.dma_start(out=tab_sb[a][:], in_=tab_words[a].rearrange("p t i -> p (t i)").bitcast(I32))
 
-        def load_w1(a, b):
-            w1_raw[a, b] = ring.tile([P, PACK, PASS], F32, name="w1raw%d%d" % (a, b), tag="raw", bufs=4)
-            rows = w1[a * PASS : (a + 1) * PASS, b * PASS : (b + 1) * PASS]
-            nc.sync.dma_start(out=w1_raw[a, b][:], in_=rows.rearrange("(p j) c -> p j c", j=PACK))
+        def load_w1_pair(a, u):
+            w1_raw[a, 0, u] = ring.tile([P, PACK, 2 * P], F32, name="w1raw%d0%d" % (a, u), tag="raw_half", bufs=6)
+            rows = w1[a * PASS : (a + 1) * PASS, 2 * P * u : 2 * P * (u + 1)]
+            nc.sync.dma_start(out=w1_raw[a, 0, u][:], in_=rows.rearrange("(p j) c -> p j c", j=PACK))
+
+        def load_w1(a):
+            if a == K_PASSES - 1:
+                w1_raw[a, 1] = ring.tile([P, PACK, PASS], F32, name="w1raw%d1" % a, tag="raw_last")
+            else:
+                w1_raw[a, 1] = ring.tile([P, PACK, PASS], F32, name="w1raw%d1" % a, tag="raw", bufs=2)
+            rows = w1[a * PASS : (a + 1) * PASS, PASS : 2 * PASS]
+            nc.sync.dma_start(out=w1_raw[a, 1][:], in_=rows.rearrange("(p j) c -> p j c", j=PACK))
 
         def load_w3(b):
-            w3_raw[b] = ring.tile([P, PACK, N], F32, name="w3raw%d" % b, tag="raw", bufs=4)
+            w3_raw[b] = ring.tile([P, PACK, N], F32, name="w3raw%d" % b, tag="raw", bufs=2)
             nc.sync.dma_start(out=w3_raw[b][:], in_=w3[b * PASS : (b + 1) * PASS, :].rearrange("(p j) n -> p j n", j=PACK))
 
         def load_wgs(t):
@@ -77,40 +86,48 @@ def tile_list_register_reread_features_kernel(
         def load_page(i):
             b, t = divmod(i, PACK)
             page[i] = ring.tile([P, T2], F32, name="page%d" % i, tag="wide", bufs=7)
-            rows = page0[b * PASS : (b + 1) * PASS, :].rearrange("(p t) c -> t p c", t=PACK)[t]
+            if b == 0:
+                rows = page0[t * P : (t + 1) * P, :]
+            else:
+                rows = page0[b * PASS : (b + 1) * PASS, :].rearrange("(p t) c -> t p c", t=PACK)[t]
             nc.sync.dma_start(out=page[i][:], in_=rows)
 
         def load_fam(b):
-            nc.sync.dma_start(out=fam_sb[b][:], in_=fam[b * PASS : (b + 1) * PASS, :].rearrange("(p t) m -> p t m", t=PACK))
+            order = "(t p) m -> p t m" if b == 0 else "(p t) m -> p t m"
+            nc.sync.dma_start(out=fam_sb[b][:], in_=fam[b * PASS : (b + 1) * PASS, :].rearrange(order, t=PACK))
 
         nc.sync.dma_start(idx[:], offs)
-        load_tab(0)
-        load_w1(0, 0)
         scale_rows = keep.tile([P, T // 4], I32, name="scale_rows")
         for q in range(P // QUAD):
             live = slice(q * QUAD, q * QUAD + PACK * K_PASSES)
-            nc.sync.dma_start(out=scale_rows[live, :], in_=tab_scales[:, PACK * q : PACK * (q + 1), :].bitcast(I32))
-        for a in range(1, K_PASSES):
-            load_tab(a)
-            load_w1(a, 0)
+            queue = nc.scalar if q % 2 == 0 else nc.sync
+            queue.dma_start(out=scale_rows[live, :], in_=tab_scales[:, PACK * q : PACK * (q + 1), :].bitcast(I32))
+        load_tab(0)
+        for a in range(K_PASSES):
+            load_w1_pair(a, 0)
+        load_tab(1)
+        load_tab(2)
         nc.sync.dma_start(idx2[:], offs2)
-        load_wgs(0)
+        nc.sync.dma_start(out=wgs_nat[:], in_=wgs)
         load_page(0)
-        load_w1(0, 1)
-        load_w1(1, 1)
-        nc.sync.dma_start(idx3[:], offs3)
-        load_wgs(1)
+        for a in range(K_PASSES):
+            load_w1_pair(a, 1)
         load_page(1)
-        load_w1(2, 1)
-        load_wgs(2)
+        nc.sync.dma_start(idx3[:], offs3)
+        load_w1(0)
+        load_w1(1)
         load_page(2)
+        load_w1(2)
+        load_wgs(0)
+        load_wgs(1)
         load_fam(0)
-        load_wgs(3)
         load_page(3)
+        load_wgs(2)
+        load_wgs(3)
         load_page(4)
         load_w3(0)
-        load_fam(1)
         load_page(5)
+        load_fam(1)
         load_w3(1)
         nc.sync.dma_start(out=w2_codes[:].bitcast(I32), in_=w2_words.rearrange("a p c -> p a c").bitcast(I32))
         for q in range(P // QUAD):
@@ -135,52 +152,45 @@ def tile_list_register_reread_features_kernel(
                     in_=tab_sb[a][:].bitcast(U32).indirect(idx[:, s * n // 16 : (s + 1) * n // 16]),
                 )
 
-        def weave_w1(a, b):
-            w1_bf[a, b] = ring.tile([P, PACK, P, PACK], BF16, name="w1bf%d%d" % (a, b), tag="bf", bufs=3, align_bytes=64)
+        for a in range(K_PASSES):
+            for b in range(R_PASSES):
+                w1_codes[a, b] = keep.tile([P, PASS], U32, name="w1c%d%d" % (a, b), align_bytes=64)
+                w1_plane[a, b] = keep.tile([P, PASS], U8, name="w1s%d%d" % (a, b), align_bytes=64)
+
+        def quantize(codes, plane, src):
+            nc.vector.quantize_mx(out=codes.bitcast(FP8X4), scales=plane, in_=src.rearrange("p c j -> p (c j)"))
+
+        def weave_w1_pair(a, u):
+            w1_bf[a, 0, u] = ring.tile([P, 2 * P, PACK], BF16, name="w1bf%d0%d" % (a, u), tag="bf", bufs=4, align_bytes=64)
             nc.scalar.copy(
-                out=w1_bf[a, b][:].rearrange("p t m j -> p m j t"),
-                in_=w1_raw[a, b][:].rearrange("p j (m t) -> p m j t", t=PACK),
+                out=w1_bf[a, 0, u][:].rearrange("p (c i) j -> p c j i", i=PACK),
+                in_=w1_raw[a, 0, u][:].rearrange("p j (c i) -> p c j i", i=PACK),
             )
 
-        def quant_w1(a, b):
-            w1_codes[a, b] = keep.tile([P, PASS], U32, name="w1c%d%d" % (a, b), align_bytes=64)
-            w1_plane[a, b] = keep.tile([P, PASS], U8, name="w1s%d%d" % (a, b), align_bytes=64)
-            nc.vector.quantize_mx(
-                out=w1_codes[a, b][:].bitcast(FP8X4),
-                scales=w1_plane[a, b][:],
-                in_=w1_bf[a, b][:].rearrange("p t m j -> p (t m j)"),
+        def quant_w1_pair(a, u):
+            cols = slice(2 * P * u, 2 * P * (u + 1))
+            quantize(w1_codes[a, 0][:, cols], w1_plane[a, 0][:, cols], w1_bf[a, 0, u][:])
+
+        def weave_w1(a):
+            w1_bf[a, 1] = ring.tile([P, PASS, PACK], BF16, name="w1bf%d1" % a, tag="bf", bufs=4, align_bytes=64)
+            nc.scalar.copy(
+                out=w1_bf[a, 1][:].rearrange("p (t m) j -> p m j t", t=PACK),
+                in_=w1_raw[a, 1][:].rearrange("p j (m t) -> p m j t", t=PACK),
             )
 
-        gather_words(0, 1)
+        def quant_w1(a):
+            quantize(w1_codes[a, 1][:], w1_plane[a, 1][:], w1_bf[a, 1][:])
+
         for q in range(P // QUAD):
             live = slice(q * QUAD, q * QUAD + PACK * K_PASSES)
             nc.vector.tensor_copy(out=tab_plane[live, :].bitcast(I32), in_=scale_rows[live, :])
         nc.vector.tensor_copy(out=v_plane[:], in_=tab_plane[:].indirect(idx[:]))
-        weave_w1(0, 0)
+        gather_words(0, 1)
+        for a in range(K_PASSES):
+            weave_w1_pair(a, 0)
+            quant_w1_pair(a, 0)
         gather_words(1, 1)
-        quant_w1(0, 0)
-        weave_w1(1, 0)
-        gather_words(2, 1)
-        quant_w1(1, 0)
-
-        last = K_PASSES - 1
-        bf_first = keep.tile([P, P, PACK], BF16, name="bf_first", align_bytes=64)
-        bf_rest = ring.tile([P, PACK - 1, P, PACK], BF16, name="bf_rest", tag="bf", bufs=3, align_bytes=64)
-        raw_last = w1_raw[last, 0][:].rearrange("p j (m t) -> p m j t", t=PACK)
-        w1_codes[last, 0] = keep.tile([P, PASS], U32, name="w1c_last", align_bytes=64)
-        w1_plane[last, 0] = keep.tile([P, PASS], U8, name="w1s_last", align_bytes=64)
-        nc.vector.tensor_copy(out=bf_first[:], in_=raw_last[:, :, :, 0])
-        nc.scalar.copy(out=bf_rest[:].rearrange("p t m j -> p m j t"), in_=raw_last[:, :, :, 1:PACK])
-        nc.vector.quantize_mx(
-            out=w1_codes[last, 0][:, 0:P].bitcast(FP8X4),
-            scales=w1_plane[last, 0][:, 0:P],
-            in_=bf_first[:].rearrange("p m j -> p (m j)"),
-        )
-        nc.vector.quantize_mx(
-            out=w1_codes[last, 0][:, P:PASS].bitcast(FP8X4),
-            scales=w1_plane[last, 0][:, P:PASS],
-            in_=bf_rest[:].rearrange("p t m j -> p (t m j)"),
-        )
+        gather_words(2, 2)
 
         h_sb = {}
 
@@ -203,78 +213,89 @@ def tile_list_register_reread_features_kernel(
                     )
                 nc.scalar.copy(out=h_sb[i][:, part], in_=acc[:])
 
-        x_rows = [keep.tile([P, PACK, M], BF16, name="x_rows0"), keep.tile([P, 2, M], BF16, name="x_rows1")]
         x_bf = [keep.tile([P, M, PACK], BF16, name="x_bf%d" % b, align_bytes=64) for b in range(R_PASSES)]
-        look_last = keep.tile([P, 2, M], F32, name="look_last")
+        look_mid = keep.tile([P, 2, M], F32, name="look_mid")
 
-        def change_page(i):
-            nc.vector.tensor_tensor(
-                out=page[i][:].indirect(idx2[:]), in0=h_sb[i][:], in1=wgs_sb[i % PACK][:], op=ALU.mult
-            )
+        def change_page(i, pieces=1):
+            weight = wgs_nat if i < PACK else wgs_sb[i - PACK]
+            n = S // pieces
+            for s in range(pieces):
+                part = slice(s * n, (s + 1) * n)
+                nc.vector.tensor_tensor(
+                    out=page[i][:].indirect(idx2[:, s * n // 16 : (s + 1) * n // 16]),
+                    in0=h_sb[i][:, part],
+                    in1=weight[:, part],
+                    op=ALU.mult,
+                )
             nc.vector.tensor_reduce(out=neg_top[i][:], in_=page[i][:], axis=AXIS.X, op=ALU.max, negate=True)
 
-        def look(i):
-            b, t = divmod(i, PACK)
-            if i >= TILES - 2:
-                looked = look_last[:, t - 2, :]
-            else:
-                looked_tile = ring.tile([P, M], F32, name="look%d" % i, tag="look", bufs=3)
-                looked = looked_tile[:]
+        def look(i, looked):
             nc.scalar.activation(out=looked, in_=page[i][:].indirect(idx3[:]), func=ACT.Exp, bias=neg_top[i][:])
-            if i < TILES - 2:
-                nc.gpsimd.tensor_tensor(out=x_rows[b][:, t, :], in0=looked, in1=fam_sb[b][:, t, :], op=ALU.mult)
 
         w3_bf = {}
 
         def weave_w3(b):
-            w3_bf[b] = ring.tile([P, N, PACK], BF16, name="w3bf%d" % b, tag="bf", bufs=3, align_bytes=64)
+            w3_bf[b] = ring.tile([P, N, PACK], BF16, name="w3bf%d" % b, tag="bf", bufs=4, align_bytes=64)
             nc.scalar.copy(
                 out=w3_bf[b][:].rearrange("p (c i) j -> p c j i", i=PACK),
                 in_=w3_raw[b][:].rearrange("p j (c i) -> p c j i", i=PACK),
             )
 
-        def quantize(codes, plane, src):
-            nc.vector.quantize_mx(out=codes.bitcast(FP8X4), scales=plane, in_=src.rearrange("p c j -> p (c j)"))
-
-        for i in range(PACK):
-            make_h(i)
+        make_h(0)
+        make_h(1)
         for a in range(K_PASSES):
-            weave_w1(a, 1)
-        change_page(0)
-        quant_w1(0, 1)
-        look(0)
+            weave_w1_pair(a, 1)
+        change_page(0, 2)
+        for a in range(K_PASSES):
+            quant_w1_pair(a, 1)
+        make_h(2)
+        make_h(3)
+        for a in range(K_PASSES):
+            weave_w1(a)
         change_page(1)
-        quant_w1(1, 1)
-        quant_w1(2, 1)
+        quant_w1(0)
+        quant_w1(1)
+        change_page(2)
+        quant_w1(2)
+        look_first = ring.tile([P, PACK, M], F32, name="look_first", tag="raw_last")
         make_h(4)
         make_h(5)
-        look(1)
-        change_page(2)
         make_h(6)
-        look(2)
+        look(0, look_first[:, 0, :])
+        look(1, look_first[:, 1, :])
+        look(2, look_first[:, 2, :])
         change_page(3)
         make_h(7)
-        look(3)
+        look(3, look_first[:, 3, :])
         weave_w3(0)
         change_page(4)
-        look(4)
+        x_nat = ring.tile([P, PACK, M], BF16, name="x_nat", tag="wgs0", align_bytes=64)
+        nc.vector.tensor_tensor(out=x_nat[:], in0=look_first[:], in1=fam_sb[0][:], op=ALU.mult)
+        look(4, look_mid[:, 0, :])
         weave_w3(1)
-        nc.scalar.copy(
-            out=x_bf[0][:].rearrange("p (c i) t -> p c t i", i=PACK),
-            in_=x_rows[0][:].rearrange("p t (c i) -> p c t i", i=PACK),
-        )
         change_page(5)
-        look(5)
+        look(5, look_mid[:, 1, :])
         w3_plane = [keep.tile([P, N], U8, name="w3s%d" % b, align_bytes=64) for b in range(R_PASSES)]
         x_plane = [keep.tile([P, M], U8, name="xs%d" % b, align_bytes=64) for b in range(R_PASSES)]
         w3_first = ring.tile([P, N], U32, name="w3c0", tag="h1", align_bytes=64)
         quantize(w3_first[:], w3_plane[0][:], w3_bf[0][:])
+        x_rows = ring.tile([P, PACK, M], BF16, name="x_rows", tag="wgs1", align_bytes=64)
+        for i in range(PACK):
+            for j in range(PACK):
+                nc.sync.dma_start(out=x_rows[i * QUAD : (i + 1) * QUAD, j, :], in_=x_nat[j:P:PACK, i, :])
+        nc.scalar.copy(
+            out=x_bf[0][:].rearrange("p (c i) t -> p c t i", i=PACK),
+            in_=x_rows[:].rearrange("p t (c i) -> p c t i", i=PACK),
+        )
         change_page(6)
-        look(6)
-        nc.scalar.copy(out=x_bf[1][:, :, 0:2], in_=x_rows[1][:].rearrange("p t m -> p m t"))
+        x_mid = ring.tile([P, 2, M], BF16, name="x_mid", tag="wgs2", align_bytes=64)
+        nc.vector.tensor_tensor(out=x_mid[:], in0=look_mid[:], in1=fam_sb[1][:, 0:2, :], op=ALU.mult)
+        look_last = ring.tile([P, 2, M], F32, name="look_last", tag="wgs1", align_bytes=64)
+        look(6, look_last[:, 0, :])
+        nc.scalar.copy(out=x_bf[1][:, :, 0:2], in_=x_mid[:].rearrange("p t m -> p m t"))
         change_page(7)
-        look(7)
-        late = ring.tile([P, 2, M], U32, name="late", tag="h3", align_bytes=64)
+        look(7, look_last[:, 1, :])
+        late = ring.tile([P, 2, M], U32, name="late", tag="wgs3", align_bytes=64)
         x_last = keep.tile([P, M], U32, name="x_last", align_bytes=64)
         x_codes = [late[:, 0, :], x_last[:]]
         w3_codes = [w3_first[:], late[:, 1, :]]
@@ -311,11 +332,11 @@ def tile_list_register_reread_features_kernel(
                     start=(b == 0),
                     stop=(b == R_PASSES - 1),
                 )
+        y_sb = ring.tile([P, N // P, M], F32, name="y_sb", tag="raw_last")
+        res = ring.tile([P, N // P, M], F32, name="res", tag="wide", bufs=7)
         for c in range(N // P):
-            y_sb = ring.tile([P, M], F32, name="ysb%d" % c, tag="look", bufs=3)
-            res = ring.tile([P, M], F32, name="res%d" % c, tag="res", bufs=4)
-            nc.scalar.copy(out=y_sb[:], in_=y_acc[c][:])
+            nc.scalar.copy(out=y_sb[:, c, :], in_=y_acc[c][:])
             nc.vector.scalar_tensor_tensor(
-                out=res[:], in0=d_acc[c][:], scalar=base_sb[:, c : c + 1], in1=y_sb[:], op0=ALU.add, op1=ALU.max
+                out=res[:, c, :], in0=d_acc[c][:], scalar=base_sb[:, c : c + 1], in1=y_sb[:, c, :], op0=ALU.add, op1=ALU.max
             )
-            nc.sync.dma_start(out=out[c * P : (c + 1) * P, :], in_=res[:])
+            nc.sync.dma_start(out=out[c * P : (c + 1) * P, :], in_=res[:, c, :])

@@ -26,6 +26,7 @@ TILES = R_PASSES * PACK
 BANK = 512
 QUAD = 32
 H_SLOTS = 4
+LAST_COLS = 256
 
 
 def tile_list_register_reread_features_kernel(
@@ -36,7 +37,7 @@ def tile_list_register_reread_features_kernel(
         lists = ctx.enter_context(tc.tile_pool(name="lists", bufs=1))
         keep = ctx.enter_context(tc.tile_pool(name="keep", bufs=1))
         ring = ctx.enter_context(tc.tile_pool(name="ring", bufs=1))
-        psum = ctx.enter_context(tc.psum_pool(name="psum", bufs=8))
+        psum = ctx.enter_context(tc.psum_pool(name="psum", bufs=1))
 
         idx = lists.tile([P, S // 16], U16, name="idx")
         idx2 = lists.tile([P, S // 16], U16, name="idx2")
@@ -46,7 +47,7 @@ def tile_list_register_reread_features_kernel(
         w2_plane = keep.tile([P, R_PASSES, N], U8, name="w2_plane", align_bytes=64)
         w2_codes = keep.tile([P, R_PASSES, 2 * N], U8, name="w2_codes", align_bytes=64)
         base_sb = keep.tile([P, N // P], F32, name="base_sb")
-        neg_top = [keep.tile([P, 1], F32, name="neg_top%d" % i) for i in range(TILES)]
+        neg_top = [keep.tile([P, 1], F32, name="neg_top%d" % i) for i in range(TILES - 2)]
         wgs_nat = keep.tile([P, S], F32, name="wgs_nat")
         wgs_sb = [ring.tile([P, S], F32, name="wgs%d" % t, tag="wgs%d" % t, align_bytes=64) for t in range(PACK)]
         fam_sb = [keep.tile([P, PACK, M], F32, name="fam%d" % b) for b in range(R_PASSES)]
@@ -60,10 +61,16 @@ def tile_list_register_reread_features_kernel(
             tab_sb[a] = ring.tile([P, T], I32, name="tab%d" % a, tag="wide", bufs=7)
             nc.sync.dma_start(out=tab_sb[a][:], in_=tab_words[a].rearrange("p t i -> p (t i)").bitcast(I32))
 
-        def load_w1_pair(a, u):
-            w1_raw[a, 0, u] = ring.tile([P, PACK, 2 * P], F32, name="w1raw%d0%d" % (a, u), tag="raw_half", bufs=6)
-            rows = w1[a * PASS : (a + 1) * PASS, 2 * P * u : 2 * P * (u + 1)]
-            nc.sync.dma_start(out=w1_raw[a, 0, u][:], in_=rows.rearrange("(p j) c -> p j c", j=PACK))
+        def load_w1_single(i):
+            w1_raw[i] = keep.tile([P, K_PASSES, PACK, P], F32, name="w1raw_single%d" % i)
+            for a in range(K_PASSES):
+                rows = w1[a * PASS : (a + 1) * PASS, P * i : P * (i + 1)]
+                nc.sync.dma_start(out=w1_raw[i][:, a, :, :], in_=rows.rearrange("(p j) c -> p j c", j=PACK))
+
+        def load_w1_pair(a):
+            w1_raw[a, 0] = keep.tile([P, PACK, 2 * P], F32, name="w1raw_pair%d" % a)
+            rows = w1[a * PASS : (a + 1) * PASS, 2 * P : 4 * P]
+            nc.sync.dma_start(out=w1_raw[a, 0][:], in_=rows.rearrange("(p j) c -> p j c", j=PACK))
 
         def load_w1(a):
             if a == K_PASSES - 1:
@@ -83,14 +90,20 @@ def tile_list_register_reread_features_kernel(
                     out=wgs_sb[t][q * QUAD : (q + 1) * QUAD, :], in_=wgs.rearrange("(g t) j -> t g j", t=PACK)[t]
                 )
 
-        def load_page(i):
+        def load_page(i, cols=slice(0, T2)):
             b, t = divmod(i, PACK)
-            page[i] = ring.tile([P, T2], F32, name="page%d" % i, tag="wide", bufs=7)
+            if cols.start == 0:
+                page[i] = ring.tile([P, T2], F32, name="page%d" % i, tag="wide", bufs=7)
             if b == 0:
                 rows = page0[t * P : (t + 1) * P, :]
             else:
                 rows = page0[b * PASS : (b + 1) * PASS, :].rearrange("(p t) c -> t p c", t=PACK)[t]
-            nc.sync.dma_start(out=page[i][:], in_=rows)
+            nc.sync.dma_start(out=page[i][:, cols], in_=rows[:, cols])
+
+        def load_page_pair(i):
+            load_page(i + 1, slice(0, T2 - LAST_COLS))
+            load_page(i)
+            load_page(i + 1, slice(T2 - LAST_COLS, T2))
 
         def load_fam(b):
             order = "(t p) m -> p t m" if b == 0 else "(p t) m -> p t m"
@@ -103,30 +116,29 @@ def tile_list_register_reread_features_kernel(
             queue = nc.scalar if q % 2 == 0 else nc.sync
             queue.dma_start(out=scale_rows[live, :], in_=tab_scales[:, PACK * q : PACK * (q + 1), :].bitcast(I32))
         load_tab(0)
-        for a in range(K_PASSES):
-            load_w1_pair(a, 0)
+        load_w1_single(0)
         load_tab(1)
         load_tab(2)
         nc.sync.dma_start(idx2[:], offs2)
-        nc.sync.dma_start(out=wgs_nat[:], in_=wgs)
+        nc.sync.dma_start(out=wgs_nat[:, 0:BANK], in_=wgs[:, 0:BANK])
         load_page(0)
-        for a in range(K_PASSES):
-            load_w1_pair(a, 1)
+        load_w1_single(1)
+        load_w1_pair(0)
+        load_w1_pair(1)
+        nc.sync.dma_start(out=wgs_nat[:, BANK:S], in_=wgs[:, BANK:S])
+        load_w1_pair(2)
         load_page(1)
         nc.sync.dma_start(idx3[:], offs3)
         load_w1(0)
         load_w1(1)
-        load_page(2)
         load_w1(2)
+        load_page_pair(2)
         load_wgs(0)
         load_wgs(1)
         load_fam(0)
-        load_page(3)
+        load_w3(0)
         load_wgs(2)
         load_wgs(3)
-        load_page(4)
-        load_w3(0)
-        load_page(5)
         load_fam(1)
         load_w3(1)
         nc.sync.dma_start(out=w2_codes[:].bitcast(I32), in_=w2_words.rearrange("a p c -> p a c").bitcast(I32))
@@ -137,8 +149,8 @@ def tile_list_register_reread_features_kernel(
             )
         with nc.allow_non_contiguous_dma(reason="one base value a partition"):
             nc.sync.dma_start(out=base_sb[:], in_=base.rearrange("(c p) -> p c", p=P))
-        load_page(6)
-        load_page(7)
+        load_page_pair(4)
+        load_page_pair(6)
 
         v_plane = keep.tile([P, S], U8, name="v_plane", align_bytes=64)
         v_codes = [keep.tile([P, S], U32, name="v_codes%d" % a, align_bytes=64) for a in range(K_PASSES)]
@@ -152,24 +164,38 @@ def tile_list_register_reread_features_kernel(
                     in_=tab_sb[a][:].bitcast(U32).indirect(idx[:, s * n // 16 : (s + 1) * n // 16]),
                 )
 
-        for a in range(K_PASSES):
-            for b in range(R_PASSES):
-                w1_codes[a, b] = keep.tile([P, PASS], U32, name="w1c%d%d" % (a, b), align_bytes=64)
-                w1_plane[a, b] = keep.tile([P, PASS], U8, name="w1s%d%d" % (a, b), align_bytes=64)
-
         def quantize(codes, plane, src):
             nc.vector.quantize_mx(out=codes.bitcast(FP8X4), scales=plane, in_=src.rearrange("p c j -> p (c j)"))
 
-        def weave_w1_pair(a, u):
-            w1_bf[a, 0, u] = ring.tile([P, 2 * P, PACK], BF16, name="w1bf%d0%d" % (a, u), tag="bf", bufs=4, align_bytes=64)
+        def weave_w1_single(i):
+            w1_bf[i] = ring.tile([P, K_PASSES * P, PACK], BF16, name="w1bf_single%d" % i, tag="bf", bufs=4, align_bytes=64)
             nc.scalar.copy(
-                out=w1_bf[a, 0, u][:].rearrange("p (c i) j -> p c j i", i=PACK),
-                in_=w1_raw[a, 0, u][:].rearrange("p j (c i) -> p c j i", i=PACK),
+                out=w1_bf[i][:].rearrange("p (a c i) j -> p a c j i", a=K_PASSES, i=PACK),
+                in_=w1_raw[i][:].rearrange("p a j (c i) -> p a c j i", i=PACK),
             )
 
-        def quant_w1_pair(a, u):
-            cols = slice(2 * P * u, 2 * P * (u + 1))
-            quantize(w1_codes[a, 0][:, cols], w1_plane[a, 0][:, cols], w1_bf[a, 0, u][:])
+        def quant_w1_single(i):
+            codes = keep.tile([P, K_PASSES * P], U32, name="w1c_single%d" % i, align_bytes=64)
+            plane = keep.tile([P, K_PASSES * P], U8, name="w1s_single%d" % i, align_bytes=64)
+            quantize(codes[:], plane[:], w1_bf[i][:])
+            for a in range(K_PASSES):
+                w1_codes[i, a] = codes[:, a * P : (a + 1) * P]
+                w1_plane[i, a] = plane[:, a * P : (a + 1) * P]
+
+        def weave_w1_pair(a):
+            w1_bf[a, 0] = ring.tile([P, 2 * P, PACK], BF16, name="w1bf_pair%d" % a, tag="bf", bufs=4, align_bytes=64)
+            nc.scalar.copy(
+                out=w1_bf[a, 0][:].rearrange("p (c i) j -> p c j i", i=PACK),
+                in_=w1_raw[a, 0][:].rearrange("p j (c i) -> p c j i", i=PACK),
+            )
+
+        def quant_w1_pair(a):
+            codes = keep.tile([P, 2 * P], U32, name="w1c_pair%d" % a, align_bytes=64)
+            plane = keep.tile([P, 2 * P], U8, name="w1s_pair%d" % a, align_bytes=64)
+            quantize(codes[:], plane[:], w1_bf[a, 0][:])
+            for u in range(2):
+                w1_codes[2 + u, a] = codes[:, u * P : (u + 1) * P]
+                w1_plane[2 + u, a] = plane[:, u * P : (u + 1) * P]
 
         def weave_w1(a):
             w1_bf[a, 1] = ring.tile([P, PASS, PACK], BF16, name="w1bf%d1" % a, tag="bf", bufs=4, align_bytes=64)
@@ -178,34 +204,35 @@ def tile_list_register_reread_features_kernel(
                 in_=w1_raw[a, 1][:].rearrange("p j (m t) -> p m j t", t=PACK),
             )
 
-        def quant_w1(a):
-            quantize(w1_codes[a, 1][:], w1_plane[a, 1][:], w1_bf[a, 1][:])
+        def quant_w1(a, plane):
+            codes = keep.tile([P, PASS], U32, name="w1c_second%d" % a, align_bytes=64)
+            quantize(codes[:], plane, w1_bf[a, 1][:])
+            for t in range(PACK):
+                w1_codes[PACK + t, a] = codes[:, t * P : (t + 1) * P]
+                w1_plane[PACK + t, a] = plane[:, t * P : (t + 1) * P]
 
         for q in range(P // QUAD):
             live = slice(q * QUAD, q * QUAD + PACK * K_PASSES)
             nc.vector.tensor_copy(out=tab_plane[live, :].bitcast(I32), in_=scale_rows[live, :])
         nc.vector.tensor_copy(out=v_plane[:], in_=tab_plane[:].indirect(idx[:]))
+        weave_w1_single(0)
         gather_words(0, 1)
-        for a in range(K_PASSES):
-            weave_w1_pair(a, 0)
-            quant_w1_pair(a, 0)
+        quant_w1_single(0)
         gather_words(1, 1)
         gather_words(2, 2)
 
         h_sb = {}
 
         def make_h(i):
-            b, t = divmod(i, PACK)
             h_sb[i] = ring.tile([P, S], F32, name="h%d" % i, tag="h%d" % (i % H_SLOTS), align_bytes=64)
-            cols = slice(t * P, (t + 1) * P)
             for s in range(S // BANK):
                 part = slice(s * BANK, (s + 1) * BANK)
-                acc = psum.tile([P, BANK], F32, name="hacc%d%d" % (i, s), tag="bank")
+                acc = psum.tile([P, BANK], F32, name="hacc%d%d" % (i, s), tag="bank%d" % (2 * (i % 4) + s))
                 for a in range(K_PASSES):
                     nc.tensor.matmul_mx(
                         out=acc[:],
-                        lhsT=w1_codes[a, b][:, cols].bitcast(FP8X4),
-                        lhsT_scale=w1_plane[a, b][:, cols],
+                        lhsT=w1_codes[i, a].bitcast(FP8X4),
+                        lhsT_scale=w1_plane[i, a],
                         rhs=v_codes[a][:, part].bitcast(FP8X4),
                         rhs_scale=v_plane[PACK * a : P, part],
                         start=(a == 0),
@@ -213,20 +240,19 @@ def tile_list_register_reread_features_kernel(
                     )
                 nc.scalar.copy(out=h_sb[i][:, part], in_=acc[:])
 
-        x_bf = [keep.tile([P, M, PACK], BF16, name="x_bf%d" % b, align_bytes=64) for b in range(R_PASSES)]
+        x_bf = [ring.tile([P, M, PACK], BF16, name="x_bf0", tag="x_bf0", align_bytes=64)]
         look_mid = keep.tile([P, 2, M], F32, name="look_mid")
 
-        def change_page(i, pieces=1):
+        def change_page(i, part=slice(0, S)):
             weight = wgs_nat if i < PACK else wgs_sb[i - PACK]
-            n = S // pieces
-            for s in range(pieces):
-                part = slice(s * n, (s + 1) * n)
-                nc.vector.tensor_tensor(
-                    out=page[i][:].indirect(idx2[:, s * n // 16 : (s + 1) * n // 16]),
-                    in0=h_sb[i][:, part],
-                    in1=weight[:, part],
-                    op=ALU.mult,
-                )
+            nc.vector.tensor_tensor(
+                out=page[i][:].indirect(idx2[:, part.start // 16 : part.stop // 16]),
+                in0=h_sb[i][:, part],
+                in1=weight[:, part],
+                op=ALU.mult,
+            )
+
+        def row_top(i):
             nc.vector.tensor_reduce(out=neg_top[i][:], in_=page[i][:], axis=AXIS.X, op=ALU.max, negate=True)
 
         def look(i, looked):
@@ -242,43 +268,50 @@ def tile_list_register_reread_features_kernel(
             )
 
         make_h(0)
+        weave_w1_single(1)
+        change_page(0, slice(0, BANK))
+        quant_w1_single(1)
         make_h(1)
         for a in range(K_PASSES):
-            weave_w1_pair(a, 1)
-        change_page(0, 2)
+            weave_w1_pair(a)
+        change_page(0, slice(BANK, S))
         for a in range(K_PASSES):
-            quant_w1_pair(a, 1)
+            quant_w1_pair(a)
+        row_top(0)
         make_h(2)
         make_h(3)
         for a in range(K_PASSES):
             weave_w1(a)
         change_page(1)
-        quant_w1(0)
-        quant_w1(1)
-        change_page(2)
-        quant_w1(2)
+        row_top(1)
         look_first = ring.tile([P, PACK, M], F32, name="look_first", tag="raw_last")
-        make_h(4)
-        make_h(5)
-        make_h(6)
         look(0, look_first[:, 0, :])
         look(1, look_first[:, 1, :])
-        look(2, look_first[:, 2, :])
+        change_page(2)
         change_page(3)
+        planes_second = ring.tile([P, K_PASSES, PASS], U8, name="planes_second", tag="h2", align_bytes=64)
+        for a in range(K_PASSES):
+            quant_w1(a, planes_second[:, a, :])
+        make_h(4)
+        make_h(5)
+        row_top(2)
+        row_top(3)
         make_h(7)
+        make_h(6)
+        look(2, look_first[:, 2, :])
         look(3, look_first[:, 3, :])
         weave_w3(0)
         change_page(4)
+        change_page(5)
         x_nat = ring.tile([P, PACK, M], BF16, name="x_nat", tag="wgs0", align_bytes=64)
         nc.vector.tensor_tensor(out=x_nat[:], in0=look_first[:], in1=fam_sb[0][:], op=ALU.mult)
+        row_top(4)
+        row_top(5)
         look(4, look_mid[:, 0, :])
-        weave_w3(1)
-        change_page(5)
         look(5, look_mid[:, 1, :])
+        weave_w3(1)
         w3_plane = [keep.tile([P, N], U8, name="w3s%d" % b, align_bytes=64) for b in range(R_PASSES)]
         x_plane = [keep.tile([P, M], U8, name="xs%d" % b, align_bytes=64) for b in range(R_PASSES)]
-        w3_first = ring.tile([P, N], U32, name="w3c0", tag="h1", align_bytes=64)
-        quantize(w3_first[:], w3_plane[0][:], w3_bf[0][:])
         x_rows = ring.tile([P, PACK, M], BF16, name="x_rows", tag="wgs1", align_bytes=64)
         for i in range(PACK):
             for j in range(PACK):
@@ -288,19 +321,29 @@ def tile_list_register_reread_features_kernel(
             in_=x_rows[:].rearrange("p t (c i) -> p c t i", i=PACK),
         )
         change_page(6)
-        x_mid = ring.tile([P, 2, M], BF16, name="x_mid", tag="wgs2", align_bytes=64)
-        nc.vector.tensor_tensor(out=x_mid[:], in0=look_mid[:], in1=fam_sb[1][:, 0:2, :], op=ALU.mult)
-        look_last = ring.tile([P, 2, M], F32, name="look_last", tag="wgs1", align_bytes=64)
-        look(6, look_last[:, 0, :])
-        nc.scalar.copy(out=x_bf[1][:, :, 0:2], in_=x_mid[:].rearrange("p t m -> p m t"))
         change_page(7)
+        x_bf.append(ring.tile([P, M, PACK], BF16, name="x_bf1", tag="wgs2", align_bytes=64))
+        nc.vector.tensor_tensor(
+            out=x_bf[1][:, :, 0:2],
+            in0=look_mid[:].rearrange("p t m -> p m t"),
+            in1=fam_sb[1][:, 0:2, :].rearrange("p t m -> p m t"),
+            op=ALU.mult,
+        )
+        last_tops = ring.tile([P, 2], F32, name="last_tops", tag="wgs1", align_bytes=64)
+        neg_top.extend([last_tops[:, 0:1], last_tops[:, 1:2]])
+        x_first = ring.tile([P, M], U32, name="x_first", tag="wgs3", align_bytes=64)
+        row_top(6)
+        quantize(x_first[:], x_plane[0][:], x_bf[0][:])
+        row_top(7)
+        look_last = keep.tile([P, 2, M], F32, name="look_last")
+        look(6, look_last[:, 0, :])
         look(7, look_last[:, 1, :])
-        late = ring.tile([P, 2, M], U32, name="late", tag="wgs3", align_bytes=64)
         x_last = keep.tile([P, M], U32, name="x_last", align_bytes=64)
-        x_codes = [late[:, 0, :], x_last[:]]
-        w3_codes = [w3_first[:], late[:, 1, :]]
-        quantize(x_codes[0], x_plane[0][:], x_bf[0][:])
-        quantize(w3_codes[1], w3_plane[1][:], w3_bf[1][:])
+        x_codes = [x_first[:], x_last[:]]
+        w3_both = ring.tile([P, R_PASSES, N], U32, name="w3_both", tag="x_bf0", align_bytes=64)
+        w3_codes = [w3_both[:, b, :] for b in range(R_PASSES)]
+        for b in range(R_PASSES):
+            quantize(w3_codes[b], w3_plane[b][:], w3_bf[b][:])
         nc.vector.tensor_tensor(
             out=x_bf[1][:, :, 2:4],
             in0=look_last[:].rearrange("p t m -> p m t"),
@@ -309,29 +352,38 @@ def tile_list_register_reread_features_kernel(
         )
         quantize(x_codes[1], x_plane[1][:], x_bf[1][:])
 
-        y_acc = [psum.tile([P, BANK], F32, name="y%d" % c, tag="bank") for c in range(N // P)]
-        d_acc = [psum.tile([P, BANK], F32, name="d%d" % c, tag="bank") for c in range(N // P)]
-        for b in range(R_PASSES):
-            for c in range(N // P):
-                cols = slice(c * P, (c + 1) * P)
-                nc.tensor.matmul_mx(
-                    out=y_acc[c][:],
-                    lhsT=w2_codes[:, b, 2 * c * P : 2 * (c + 1) * P].bitcast(FP4X4),
-                    lhsT_scale=w2_plane[:, b, cols],
-                    rhs=x_codes[b].bitcast(FP8X4),
-                    rhs_scale=x_plane[b][:],
-                    start=(b == 0),
-                    stop=(b == R_PASSES - 1),
-                )
-                nc.tensor.matmul_mx(
-                    out=d_acc[c][:],
-                    lhsT=w3_codes[b][:, cols].bitcast(FP8X4),
-                    lhsT_scale=w3_plane[b][:, cols],
-                    rhs=x_codes[b].bitcast(FP8X4),
-                    rhs_scale=x_plane[b][:],
-                    start=(b == 0),
-                    stop=(b == R_PASSES - 1),
-                )
+        y_acc = [psum.tile([P, BANK], F32, name="y%d" % c, tag="bank%d" % (2 * c)) for c in range(N // P)]
+        d_acc = [psum.tile([P, BANK], F32, name="d%d" % c, tag="bank%d" % (2 * c + 1)) for c in range(N // P)]
+
+        def y_pass(b, c):
+            nc.tensor.matmul_mx(
+                out=y_acc[c][:],
+                lhsT=w2_codes[:, b, 2 * c * P : 2 * (c + 1) * P].bitcast(FP4X4),
+                lhsT_scale=w2_plane[:, b, c * P : (c + 1) * P],
+                rhs=x_codes[b].bitcast(FP8X4),
+                rhs_scale=x_plane[b][:],
+                start=(b == 0),
+                stop=(b == R_PASSES - 1),
+            )
+
+        def d_pass(b, c):
+            nc.tensor.matmul_mx(
+                out=d_acc[c][:],
+                lhsT=w3_codes[b][:, c * P : (c + 1) * P].bitcast(FP8X4),
+                lhsT_scale=w3_plane[b][:, c * P : (c + 1) * P],
+                rhs=x_codes[b].bitcast(FP8X4),
+                rhs_scale=x_plane[b][:],
+                start=(b == 0),
+                stop=(b == R_PASSES - 1),
+            )
+
+        for c in range(N // P):
+            y_pass(0, c)
+        for c in range(N // P):
+            d_pass(0, c)
+        for c in range(N // P):
+            y_pass(1, c)
+            d_pass(1, c)
         y_sb = ring.tile([P, N // P, M], F32, name="y_sb", tag="raw_last")
         res = ring.tile([P, N // P, M], F32, name="res", tag="wide", bufs=7)
         for c in range(N // P):

@@ -47,7 +47,7 @@ def tile_list_register_reread_features_kernel(
         w2_plane = keep.tile([P, R_PASSES, N], U8, name="w2_plane", align_bytes=64)
         w2_codes = keep.tile([P, R_PASSES, 2 * N], U8, name="w2_codes", align_bytes=64)
         base_sb = keep.tile([P, N // P], F32, name="base_sb")
-        neg_top = [keep.tile([P, 1], F32, name="neg_top%d" % i) for i in range(TILES - 2)]
+        neg_top = {i: keep.tile([P, 1], F32, name="neg_top%d" % i) for i in (0, 1, 4, 5)}
         wgs_nat = keep.tile([P, S], F32, name="wgs_nat")
         wgs_sb = [ring.tile([P, S], F32, name="wgs%d" % t, tag="wgs%d" % t, align_bytes=64) for t in range(PACK)]
         fam_sb = [keep.tile([P, PACK, M], F32, name="fam%d" % b) for b in range(R_PASSES)]
@@ -61,16 +61,10 @@ def tile_list_register_reread_features_kernel(
             tab_sb[a] = ring.tile([P, T], I32, name="tab%d" % a, tag="wide", bufs=7)
             nc.sync.dma_start(out=tab_sb[a][:], in_=tab_words[a].rearrange("p t i -> p (t i)").bitcast(I32))
 
-        def load_w1_single(i):
-            w1_raw[i] = keep.tile([P, K_PASSES, PACK, P], F32, name="w1raw_single%d" % i)
-            for a in range(K_PASSES):
-                rows = w1[a * PASS : (a + 1) * PASS, P * i : P * (i + 1)]
-                nc.sync.dma_start(out=w1_raw[i][:, a, :, :], in_=rows.rearrange("(p j) c -> p j c", j=PACK))
-
-        def load_w1_pair(a):
-            w1_raw[a, 0] = keep.tile([P, PACK, 2 * P], F32, name="w1raw_pair%d" % a)
-            rows = w1[a * PASS : (a + 1) * PASS, 2 * P : 4 * P]
-            nc.sync.dma_start(out=w1_raw[a, 0][:], in_=rows.rearrange("(p j) c -> p j c", j=PACK))
+        def load_w1_pair(a, u):
+            w1_raw[a, 0, u] = keep.tile([P, PACK, 2 * P], F32, name="w1raw_pair%d%d" % (a, u))
+            rows = w1[a * PASS : (a + 1) * PASS, 2 * P * u : 2 * P * (u + 1)]
+            nc.sync.dma_start(out=w1_raw[a, 0, u][:], in_=rows.rearrange("(p j) c -> p j c", j=PACK))
 
         def load_w1(a):
             if a == K_PASSES - 1:
@@ -116,29 +110,30 @@ def tile_list_register_reread_features_kernel(
             queue = nc.scalar if q % 2 == 0 else nc.sync
             queue.dma_start(out=scale_rows[live, :], in_=tab_scales[:, PACK * q : PACK * (q + 1), :].bitcast(I32))
         load_tab(0)
-        load_w1_single(0)
+        load_w1_pair(0, 0)
         load_tab(1)
+        load_w1_pair(1, 0)
+        load_w1_pair(2, 0)
         load_tab(2)
         nc.sync.dma_start(idx2[:], offs2)
         nc.sync.dma_start(out=wgs_nat[:, 0:BANK], in_=wgs[:, 0:BANK])
         load_page(0)
-        load_w1_single(1)
-        load_w1_pair(0)
-        load_w1_pair(1)
         nc.sync.dma_start(out=wgs_nat[:, BANK:S], in_=wgs[:, BANK:S])
-        load_w1_pair(2)
+        for a in range(K_PASSES):
+            load_w1_pair(a, 1)
         load_page(1)
         nc.sync.dma_start(idx3[:], offs3)
-        load_w1(0)
-        load_w1(1)
-        load_w1(2)
         load_page_pair(2)
+        for a in range(K_PASSES):
+            load_w1(a)
         load_wgs(0)
         load_wgs(1)
+        load_page_pair(4)
         load_fam(0)
-        load_w3(0)
         load_wgs(2)
         load_wgs(3)
+        load_page_pair(6)
+        load_w3(0)
         load_fam(1)
         load_w3(1)
         nc.sync.dma_start(out=w2_codes[:].bitcast(I32), in_=w2_words.rearrange("a p c -> p a c").bitcast(I32))
@@ -149,8 +144,6 @@ def tile_list_register_reread_features_kernel(
             )
         with nc.allow_non_contiguous_dma(reason="one base value a partition"):
             nc.sync.dma_start(out=base_sb[:], in_=base.rearrange("(c p) -> p c", p=P))
-        load_page_pair(4)
-        load_page_pair(6)
 
         v_plane = keep.tile([P, S], U8, name="v_plane", align_bytes=64)
         v_codes = [keep.tile([P, S], U32, name="v_codes%d" % a, align_bytes=64) for a in range(K_PASSES)]
@@ -167,38 +160,26 @@ def tile_list_register_reread_features_kernel(
         def quantize(codes, plane, src):
             nc.vector.quantize_mx(out=codes.bitcast(FP8X4), scales=plane, in_=src.rearrange("p c j -> p (c j)"))
 
-        def weave_w1_single(i):
-            w1_bf[i] = ring.tile([P, K_PASSES * P, PACK], BF16, name="w1bf_single%d" % i, tag="bf", bufs=4, align_bytes=64)
+        def weave_w1_pair(a, u):
+            w1_bf[a, 0, u] = ring.tile([P, 2 * P, PACK], BF16, name="w1bf_pair%d%d" % (a, u), tag="bf", bufs=4, align_bytes=64)
             nc.scalar.copy(
-                out=w1_bf[i][:].rearrange("p (a c i) j -> p a c j i", a=K_PASSES, i=PACK),
-                in_=w1_raw[i][:].rearrange("p a j (c i) -> p a c j i", i=PACK),
+                out=w1_bf[a, 0, u][:].rearrange("p (c i) j -> p c j i", i=PACK),
+                in_=w1_raw[a, 0, u][:].rearrange("p j (c i) -> p c j i", i=PACK),
             )
 
-        def quant_w1_single(i):
-            codes = keep.tile([P, K_PASSES * P], U32, name="w1c_single%d" % i, align_bytes=64)
-            plane = keep.tile([P, K_PASSES * P], U8, name="w1s_single%d" % i, align_bytes=64)
-            quantize(codes[:], plane[:], w1_bf[i][:])
-            for a in range(K_PASSES):
-                w1_codes[i, a] = codes[:, a * P : (a + 1) * P]
-                w1_plane[i, a] = plane[:, a * P : (a + 1) * P]
-
-        def weave_w1_pair(a):
-            w1_bf[a, 0] = ring.tile([P, 2 * P, PACK], BF16, name="w1bf_pair%d" % a, tag="bf", bufs=4, align_bytes=64)
-            nc.scalar.copy(
-                out=w1_bf[a, 0][:].rearrange("p (c i) j -> p c j i", i=PACK),
-                in_=w1_raw[a, 0][:].rearrange("p j (c i) -> p c j i", i=PACK),
-            )
-
-        def quant_w1_pair(a):
-            codes = keep.tile([P, 2 * P], U32, name="w1c_pair%d" % a, align_bytes=64)
-            plane = keep.tile([P, 2 * P], U8, name="w1s_pair%d" % a, align_bytes=64)
-            quantize(codes[:], plane[:], w1_bf[a, 0][:])
-            for u in range(2):
-                w1_codes[2 + u, a] = codes[:, u * P : (u + 1) * P]
-                w1_plane[2 + u, a] = plane[:, u * P : (u + 1) * P]
+        def quant_w1_pair(a, u):
+            codes = keep.tile([P, 2 * P], U32, name="w1c_pair%d%d" % (a, u), align_bytes=64)
+            plane = keep.tile([P, 2 * P], U8, name="w1s_pair%d%d" % (a, u), align_bytes=64)
+            quantize(codes[:], plane[:], w1_bf[a, 0, u][:])
+            for e in range(2):
+                w1_codes[2 * u + e, a] = codes[:, e * P : (e + 1) * P]
+                w1_plane[2 * u + e, a] = plane[:, e * P : (e + 1) * P]
 
         def weave_w1(a):
-            w1_bf[a, 1] = ring.tile([P, PASS, PACK], BF16, name="w1bf%d1" % a, tag="bf", bufs=4, align_bytes=64)
+            if a == K_PASSES - 1:
+                w1_bf[a, 1] = ring.tile([P, PASS, PACK], BF16, name="w1bf%d1" % a, tag="bf_last", align_bytes=64)
+            else:
+                w1_bf[a, 1] = ring.tile([P, PASS, PACK], BF16, name="w1bf%d1" % a, tag="bf", bufs=4, align_bytes=64)
             nc.scalar.copy(
                 out=w1_bf[a, 1][:].rearrange("p (t m) j -> p m j t", t=PACK),
                 in_=w1_raw[a, 1][:].rearrange("p j (m t) -> p m j t", t=PACK),
@@ -215,10 +196,13 @@ def tile_list_register_reread_features_kernel(
             live = slice(q * QUAD, q * QUAD + PACK * K_PASSES)
             nc.vector.tensor_copy(out=tab_plane[live, :].bitcast(I32), in_=scale_rows[live, :])
         nc.vector.tensor_copy(out=v_plane[:], in_=tab_plane[:].indirect(idx[:]))
-        weave_w1_single(0)
+        for a in range(K_PASSES):
+            weave_w1_pair(a, 0)
         gather_words(0, 1)
-        quant_w1_single(0)
+        quant_w1_pair(0, 0)
         gather_words(1, 1)
+        quant_w1_pair(1, 0)
+        quant_w1_pair(2, 0)
         gather_words(2, 2)
 
         h_sb = {}
@@ -227,7 +211,7 @@ def tile_list_register_reread_features_kernel(
             h_sb[i] = ring.tile([P, S], F32, name="h%d" % i, tag="h%d" % (i % H_SLOTS), align_bytes=64)
             for s in range(S // BANK):
                 part = slice(s * BANK, (s + 1) * BANK)
-                acc = psum.tile([P, BANK], F32, name="hacc%d%d" % (i, s), tag="bank%d" % (2 * (i % 4) + s))
+                acc = psum.tile([P, BANK], F32, name="hacc%d%d" % (i, s), tag="bank%d" % (2 * min(max(i - 1, 0), 3) + s))
                 for a in range(K_PASSES):
                     nc.tensor.matmul_mx(
                         out=acc[:],
@@ -268,15 +252,13 @@ def tile_list_register_reread_features_kernel(
             )
 
         make_h(0)
-        weave_w1_single(1)
-        change_page(0, slice(0, BANK))
-        quant_w1_single(1)
         make_h(1)
         for a in range(K_PASSES):
-            weave_w1_pair(a)
+            weave_w1_pair(a, 1)
+        change_page(0, slice(0, BANK))
         change_page(0, slice(BANK, S))
         for a in range(K_PASSES):
-            quant_w1_pair(a)
+            quant_w1_pair(a, 1)
         row_top(0)
         make_h(2)
         make_h(3)
@@ -294,6 +276,8 @@ def tile_list_register_reread_features_kernel(
             quant_w1(a, planes_second[:, a, :])
         make_h(4)
         make_h(5)
+        mid_tops = ring.tile([P, 2], F32, name="mid_tops", tag="bf_last", align_bytes=64)
+        neg_top[2], neg_top[3] = mid_tops[:, 0:1], mid_tops[:, 1:2]
         row_top(2)
         row_top(3)
         make_h(7)
@@ -330,7 +314,7 @@ def tile_list_register_reread_features_kernel(
             op=ALU.mult,
         )
         last_tops = ring.tile([P, 2], F32, name="last_tops", tag="wgs1", align_bytes=64)
-        neg_top.extend([last_tops[:, 0:1], last_tops[:, 1:2]])
+        neg_top[6], neg_top[7] = last_tops[:, 0:1], last_tops[:, 1:2]
         x_first = ring.tile([P, M], U32, name="x_first", tag="wgs3", align_bytes=64)
         row_top(6)
         quantize(x_first[:], x_plane[0][:], x_bf[0][:])

@@ -126,10 +126,10 @@ def tile_list_register_reread_features_kernel(
         load_page_pair(2)
         for a in range(K_PASSES):
             load_w1(a)
+        load_fam(0)
         load_wgs(0)
         load_wgs(1)
         load_page_pair(4)
-        load_fam(0)
         load_wgs(2)
         load_wgs(3)
         load_page_pair(6)
@@ -161,7 +161,7 @@ def tile_list_register_reread_features_kernel(
             nc.vector.quantize_mx(out=codes.bitcast(FP8X4), scales=plane, in_=src.rearrange("p c j -> p (c j)"))
 
         def weave_w1_pair(a, u):
-            w1_bf[a, 0, u] = ring.tile([P, 2 * P, PACK], BF16, name="w1bf_pair%d%d" % (a, u), tag="bf", bufs=4, align_bytes=64)
+            w1_bf[a, 0, u] = ring.tile([P, 2 * P, PACK], BF16, name="w1bf_pair%d%d" % (a, u), tag="bf", bufs=3, align_bytes=64)
             nc.scalar.copy(
                 out=w1_bf[a, 0, u][:].rearrange("p (c i) j -> p c j i", i=PACK),
                 in_=w1_raw[a, 0, u][:].rearrange("p j (c i) -> p c j i", i=PACK),
@@ -176,10 +176,10 @@ def tile_list_register_reread_features_kernel(
                 w1_plane[2 * u + e, a] = plane[:, e * P : (e + 1) * P]
 
         def weave_w1(a):
-            if a == K_PASSES - 1:
-                w1_bf[a, 1] = ring.tile([P, PASS, PACK], BF16, name="w1bf%d1" % a, tag="bf_last", align_bytes=64)
+            if a > 0:
+                w1_bf[a, 1] = ring.tile([P, PASS, PACK], BF16, name="w1bf%d1" % a, tag="bf_own%d" % a, align_bytes=64)
             else:
-                w1_bf[a, 1] = ring.tile([P, PASS, PACK], BF16, name="w1bf%d1" % a, tag="bf", bufs=4, align_bytes=64)
+                w1_bf[a, 1] = ring.tile([P, PASS, PACK], BF16, name="w1bf%d1" % a, tag="bf", bufs=3, align_bytes=64)
             nc.scalar.copy(
                 out=w1_bf[a, 1][:].rearrange("p (t m) j -> p m j t", t=PACK),
                 in_=w1_raw[a, 1][:].rearrange("p j (m t) -> p m j t", t=PACK),
@@ -245,7 +245,7 @@ def tile_list_register_reread_features_kernel(
         w3_bf = {}
 
         def weave_w3(b):
-            w3_bf[b] = ring.tile([P, N, PACK], BF16, name="w3bf%d" % b, tag="bf", bufs=4, align_bytes=64)
+            w3_bf[b] = ring.tile([P, N, PACK], BF16, name="w3bf%d" % b, tag="bf", bufs=3, align_bytes=64)
             nc.scalar.copy(
                 out=w3_bf[b][:].rearrange("p (c i) j -> p c j i", i=PACK),
                 in_=w3_raw[b][:].rearrange("p j (c i) -> p c j i", i=PACK),
@@ -274,9 +274,11 @@ def tile_list_register_reread_features_kernel(
         planes_second = ring.tile([P, K_PASSES, PASS], U8, name="planes_second", tag="h2", align_bytes=64)
         for a in range(K_PASSES):
             quant_w1(a, planes_second[:, a, :])
+        x_nat = [ring.tile([P, 2, M], BF16, name="x_nat0", tag="bf_own1", align_bytes=64)]
+        nc.gpsimd.tensor_tensor(out=x_nat[0][:], in0=look_first[:, 0:2, :], in1=fam_sb[0][:, 0:2, :], op=ALU.mult)
         make_h(4)
         make_h(5)
-        mid_tops = ring.tile([P, 2], F32, name="mid_tops", tag="bf_last", align_bytes=64)
+        mid_tops = ring.tile([P, 2], F32, name="mid_tops", tag="bf_own2", align_bytes=64)
         neg_top[2], neg_top[3] = mid_tops[:, 0:1], mid_tops[:, 1:2]
         row_top(2)
         row_top(3)
@@ -287,8 +289,8 @@ def tile_list_register_reread_features_kernel(
         weave_w3(0)
         change_page(4)
         change_page(5)
-        x_nat = ring.tile([P, PACK, M], BF16, name="x_nat", tag="wgs0", align_bytes=64)
-        nc.vector.tensor_tensor(out=x_nat[:], in0=look_first[:], in1=fam_sb[0][:], op=ALU.mult)
+        x_nat.append(ring.tile([P, 2, M], BF16, name="x_nat1", tag="h1", align_bytes=64))
+        nc.gpsimd.tensor_tensor(out=x_nat[1][:], in0=look_first[:, 2:4, :], in1=fam_sb[0][:, 2:4, :], op=ALU.mult)
         row_top(4)
         row_top(5)
         look(4, look_mid[:, 0, :])
@@ -299,20 +301,17 @@ def tile_list_register_reread_features_kernel(
         x_rows = ring.tile([P, PACK, M], BF16, name="x_rows", tag="wgs1", align_bytes=64)
         for i in range(PACK):
             for j in range(PACK):
-                nc.sync.dma_start(out=x_rows[i * QUAD : (i + 1) * QUAD, j, :], in_=x_nat[j:P:PACK, i, :])
+                nc.sync.dma_start(out=x_rows[i * QUAD : (i + 1) * QUAD, j, :], in_=x_nat[i // 2][j:P:PACK, i % 2, :])
         nc.scalar.copy(
             out=x_bf[0][:].rearrange("p (c i) t -> p c t i", i=PACK),
             in_=x_rows[:].rearrange("p t (c i) -> p c t i", i=PACK),
         )
         change_page(6)
         change_page(7)
-        x_bf.append(ring.tile([P, M, PACK], BF16, name="x_bf1", tag="wgs2", align_bytes=64))
-        nc.vector.tensor_tensor(
-            out=x_bf[1][:, :, 0:2],
-            in0=look_mid[:].rearrange("p t m -> p m t"),
-            in1=fam_sb[1][:, 0:2, :].rearrange("p t m -> p m t"),
-            op=ALU.mult,
-        )
+        x_mid = ring.tile([P, 2, M], BF16, name="x_mid", tag="wgs2", align_bytes=64)
+        nc.vector.tensor_tensor(out=x_mid[:], in0=look_mid[:], in1=fam_sb[1][:, 0:2, :], op=ALU.mult)
+        x_bf.append(ring.tile([P, M, PACK], BF16, name="x_bf1", tag="h1", align_bytes=64))
+        nc.scalar.copy(out=x_bf[1][:, :, 0:2], in_=x_mid[:].rearrange("p t m -> p m t"))
         last_tops = ring.tile([P, 2], F32, name="last_tops", tag="wgs1", align_bytes=64)
         neg_top[6], neg_top[7] = last_tops[:, 0:1], last_tops[:, 1:2]
         x_first = ring.tile([P, M], U32, name="x_first", tag="wgs3", align_bytes=64)

from contextlib import ExitStack

import concourse.mybir as mybir

K, H, N, T, S, T2, M = 1536, 1024, 512, 2048, 1024, 2048, 512
FLOPS = 2 * K * H * S + 2 * 2 * H * N * M

F32 = mybir.dt.float32
BF16 = mybir.dt.bfloat16
I32 = mybir.dt.int32
U32 = mybir.dt.uint32
U16 = mybir.dt.uint16
U8 = mybir.dt.uint8
FP8X4 = mybir.dt.float8_e4m3fn_x4
FP4X4 = mybir.dt.float4_e2m1fn_x4
ALU = mybir.AluOpType
ACT = mybir.ActivationFunctionType
AXIS = mybir.AxisListType

P = 128
PACK = 4
PASS = P * PACK
K_PASSES = K // PASS
R_PASSES = H // PASS
TILES = R_PASSES * PACK
BANK = 512
QUAD = 32
H_SLOTS = 4
LAST_COLS = 256


def tile_list_register_reread_features_kernel(
    tc, tab_words, tab_scales, offs, offs2, offs3, w1, wgs, page0, fam, w2_words, w2_scales, w3, base, out
):
    nc = tc.nc
    with ExitStack() as ctx:
        lists = ctx.enter_context(tc.tile_pool(name="lists", bufs=1))
        keep = ctx.enter_context(tc.tile_pool(name="keep", bufs=1))
        ring = ctx.enter_context(tc.tile_pool(name="ring", bufs=1))
        psum = ctx.enter_context(tc.psum_pool(name="psum", bufs=1))

        idx = lists.tile([P, S // 16], U16, name="idx")
        idx2 = lists.tile([P, S // 16], U16, name="idx2")
        idx3 = lists.tile([P, M // 16], U16, name="idx3")

        tab_plane = keep.tile([P, T], U8, name="tab_plane", align_bytes=64)
        w2_plane = keep.tile([P, R_PASSES, N], U8, name="w2_plane", align_bytes=64)
        w2_codes = keep.tile([P, R_PASSES, 2 * N], U8, name="w2_codes", align_bytes=64)
        base_sb = keep.tile([P, N // P], F32, name="base_sb")
        neg_top = {i: keep.tile([P, 1], F32, name="neg_top%d" % i) for i in (0, 1, 4, 5)}
        wgs_nat = keep.tile([P, S], F32, name="wgs_nat")
        wgs_sb = [ring.tile([P, S], F32, name="wgs%d" % t, tag="wgs%d" % t, align_bytes=64) for t in range(PACK)]
        fam_sb = [keep.tile([P, PACK, M], F32, name="fam%d" % b) for b in range(R_PASSES)]

        nc.vector.memset(tab_plane[:].bitcast(I32), 0)
        nc.vector.memset(w2_plane[:].rearrange("p a n -> p (a n)").bitcast(I32), 0)

        tab_sb, w1_raw, w3_raw, page = {}, {}, {}, {}

        def load_tab(a):
            tab_sb[a] = ring.tile([P, T], I32, name="tab%d" % a, tag="wide", bufs=7)
            nc.sync.dma_start(out=tab_sb[a][:], in_=tab_words[a].rearrange("p t i -> p (t i)").bitcast(I32))

        def load_w1_pair(a, u):
            w1_raw[a, 0, u] = keep.tile([P, PACK, 2 * P], F32, name="w1raw_pair%d%d" % (a, u))
            rows = w1[a * PASS : (a + 1) * PASS, 2 * P * u : 2 * P * (u + 1)]
            nc.sync.dma_start(out=w1_raw[a, 0, u][:], in_=rows.rearrange("(p j) c -> p j c", j=PACK))

        def load_w1(a):
            if a == K_PASSES - 1:
                w1_raw[a, 1] = ring.tile([P, PACK, PASS], F32, name="w1raw%d1" % a, tag="raw_last")
            else:
                w1_raw[a, 1] = ring.tile([P, PACK, PASS], F32, name="w1raw%d1" % a, tag="raw", bufs=2)
            rows = w1[a * PASS : (a + 1) * PASS, PASS : 2 * PASS]
            nc.sync.dma_start(out=w1_raw[a, 1][:], in_=rows.rearrange("(p j) c -> p j c", j=PACK))

        def load_w3(b):
            w3_raw[b] = ring.tile([P, PACK, N], F32, name="w3raw%d" % b, tag="raw", bufs=2)
            nc.sync.dma_start(out=w3_raw[b][:], in_=w3[b * PASS : (b + 1) * PASS, :].rearrange("(p j) n -> p j n", j=PACK))

        def load_wgs(t):
            for q in range(P // QUAD):
                nc.sync.dma_start(
                    out=wgs_sb[t][q * QUAD : (q + 1) * QUAD, :], in_=wgs.rearrange("(g t) j -> t g j", t=PACK)[t]
                )

        def load_page(i, cols=slice(0, T2)):
            b, t = divmod(i, PACK)
            if cols.start == 0:
                page[i] = ring.tile([P, T2], F32, name="page%d" % i, tag="wide", bufs=7)
            if b == 0:
                rows = page0[t * P : (t + 1) * P, :]
            else:
                rows = page0[b * PASS : (b + 1) * PASS, :].rearrange("(p t) c -> t p c", t=PACK)[t]
            nc.sync.dma_start(out=page[i][:, cols], in_=rows[:, cols])

        def load_page_pair(i):
            load_page(i + 1, slice(0, T2 - LAST_COLS))
            load_page(i)
            load_page(i + 1, slice(T2 - LAST_COLS, T2))

        def load_fam(b):
            order = "(t p) m -> p t m" if b == 0 else "(p t) m -> p t m"
            nc.sync.dma_start(out=fam_sb[b][:], in_=fam[b * PASS : (b + 1) * PASS, :].rearrange(order, t=PACK))

        nc.sync.dma_start(idx[:], offs)
        scale_rows = keep.tile([P, T // 4], I32, name="scale_rows")
        for q in range(P // QUAD):
            live = slice(q * QUAD, q * QUAD + PACK * K_PASSES)
            queue = nc.scalar if q % 2 == 0 else nc.sync
            queue.dma_start(out=scale_rows[live, :], in_=tab_scales[:, PACK * q : PACK * (q + 1), :].bitcast(I32))
        load_tab(0)
        load_w1_pair(0, 0)
        load_tab(1)
        load_w1_pair(1, 0)
        load_w1_pair(2, 0)
        load_tab(2)
        nc.sync.dma_start(idx2[:], offs2)
        nc.sync.dma_start(out=wgs_nat[:, 0:BANK], in_=wgs[:, 0:BANK])
        load_page(0)
        nc.sync.dma_start(out=wgs_nat[:, BANK:S], in_=wgs[:, BANK:S])
        for a in range(K_PASSES):
            load_w1_pair(a, 1)
        load_page(1)
        nc.sync.dma_start(idx3[:], offs3)
        load_page_pair(2)
        for a in range(K_PASSES):
            load_w1(a)
        load_fam(0)
        load_wgs(0)
        load_wgs(1)
        load_page_pair(4)
        load_wgs(2)
        load_wgs(3)
        load_page_pair(6)
        load_w3(0)
        load_fam(1)
        load_w3(1)
        nc.sync.dma_start(out=w2_codes[:].bitcast(I32), in_=w2_words.rearrange("a p c -> p a c").bitcast(I32))
        for q in range(P // QUAD):
            nc.sync.dma_start(
                out=w2_plane[q * QUAD : q * QUAD + PACK, :, :].bitcast(I32),
                in_=w2_scales[:, PACK * q : PACK * (q + 1), :].rearrange("a r n -> r a n").bitcast(I32),
            )
        with nc.allow_non_contiguous_dma(reason="one base value a partition"):
            nc.sync.dma_start(out=base_sb[:], in_=base.rearrange("(c p) -> p c", p=P))

        v_plane = keep.tile([P, S], U8, name="v_plane", align_bytes=64)
        v_codes = [keep.tile([P, S], U32, name="v_codes%d" % a, align_bytes=64) for a in range(K_PASSES)]
        w1_codes, w1_plane, w1_bf = {}, {}, {}

        def gather_words(a, pieces):
            n = S // pieces
            for s in range(pieces):
                nc.vector.tensor_copy(
                    out=v_codes[a][:, s * n : (s + 1) * n],
                    in_=tab_sb[a][:].bitcast(U32).indirect(idx[:, s * n // 16 : (s + 1) * n // 16]),
                )

        def quantize(codes, plane, src):
            nc.vector.quantize_mx(out=codes.bitcast(FP8X4), scales=plane, in_=src.rearrange("p c j -> p (c j)"))

        def weave_w1_pair(a, u):
            w1_bf[a, 0, u] = ring.tile([P, 2 * P, PACK], BF16, name="w1bf_pair%d%d" % (a, u), tag="bf", bufs=3, align_bytes=64)
            nc.scalar.copy(
                out=w1_bf[a, 0, u][:].rearrange("p (c i) j -> p c j i", i=PACK),
                in_=w1_raw[a, 0, u][:].rearrange("p j (c i) -> p c j i", i=PACK),
            )

        def quant_w1_pair(a, u):
            codes = keep.tile([P, 2 * P], U32, name="w1c_pair%d%d" % (a, u), align_bytes=64)
            plane = keep.tile([P, 2 * P], U8, name="w1s_pair%d%d" % (a, u), align_bytes=64)
            quantize(codes[:], plane[:], w1_bf[a, 0, u][:])
            for e in range(2):
                w1_codes[2 * u + e, a] = codes[:, e * P : (e + 1) * P]
                w1_plane[2 * u + e, a] = plane[:, e * P : (e + 1) * P]

        def weave_w1(a):
            if a > 0:
                w1_bf[a, 1] = ring.tile([P, PASS, PACK], BF16, name="w1bf%d1" % a, tag="bf_own%d" % a, align_bytes=64)
            else:
                w1_bf[a, 1] = ring.tile([P, PASS, PACK], BF16, name="w1bf%d1" % a, tag="bf", bufs=3, align_bytes=64)
            nc.scalar.copy(
                out=w1_bf[a, 1][:].rearrange("p (t m) j -> p m j t", t=PACK),
                in_=w1_raw[a, 1][:].rearrange("p j (m t) -> p m j t", t=PACK),
            )

        def quant_w1(a, plane):
            codes = keep.tile([P, PASS], U32, name="w1c_second%d" % a, align_bytes=64)
            quantize(codes[:], plane, w1_bf[a, 1][:])
            for t in range(PACK):
                w1_codes[PACK + t, a] = codes[:, t * P : (t + 1) * P]
                w1_plane[PACK + t, a] = plane[:, t * P : (t + 1) * P]

        for q in range(P // QUAD):
            live = slice(q * QUAD, q * QUAD + PACK * K_PASSES)
            nc.vector.tensor_copy(out=tab_plane[live, :].bitcast(I32), in_=scale_rows[live, :])
        nc.vector.tensor_copy(out=v_plane[:], in_=tab_plane[:].indirect(idx[:]))
        for a in range(K_PASSES):
            weave_w1_pair(a, 0)
        gather_words(0, 1)
        quant_w1_pair(0, 0)
        gather_words(1, 1)
        quant_w1_pair(1, 0)
        quant_w1_pair(2, 0)
        gather_words(2, 2)

        h_sb = {}

        def make_h(i):
            h_sb[i] = ring.tile([P, S], F32, name="h%d" % i, tag="h%d" % (i % H_SLOTS), align_bytes=64)
            for s in range(S // BANK):
                part = slice(s * BANK, (s + 1) * BANK)
                acc = psum.tile([P, BANK], F32, name="hacc%d%d" % (i, s), tag="bank%d" % (2 * min(max(i - 1, 0), 3) + s))
                for a in range(K_PASSES):
                    nc.tensor.matmul_mx(
                        out=acc[:],
                        lhsT=w1_codes[i, a].bitcast(FP8X4),
                        lhsT_scale=w1_plane[i, a],
                        rhs=v_codes[a][:, part].bitcast(FP8X4),
                        rhs_scale=v_plane[PACK * a : P, part],
                        start=(a == 0),
                        stop=(a == K_PASSES - 1),
                    )
                nc.scalar.copy(out=h_sb[i][:, part], in_=acc[:])

        x_bf = [ring.tile([P, M, PACK], BF16, name="x_bf0", tag="x_bf0", align_bytes=64)]
        look_mid = keep.tile([P, 2, M], F32, name="look_mid")

        def change_page(i, part=slice(0, S)):
            weight = wgs_nat if i < PACK else wgs_sb[i - PACK]
            nc.vector.tensor_tensor(
                out=page[i][:].indirect(idx2[:, part.start // 16 : part.stop // 16]),
                in0=h_sb[i][:, part],
                in1=weight[:, part],
                op=ALU.mult,
            )

        def row_top(i):
            nc.vector.tensor_reduce(out=neg_top[i][:], in_=page[i][:], axis=AXIS.X, op=ALU.max, negate=True)

        def look(i, looked):
            nc.scalar.activation(out=looked, in_=page[i][:].indirect(idx3[:]), func=ACT.Exp, bias=neg_top[i][:])

        w3_bf = {}

        def weave_w3(b):
            w3_bf[b] = ring.tile([P, N, PACK], BF16, name="w3bf%d" % b, tag="bf", bufs=3, align_bytes=64)
            nc.scalar.copy(
                out=w3_bf[b][:].rearrange("p (c i) j -> p c j i", i=PACK),
                in_=w3_raw[b][:].rearrange("p j (c i) -> p c j i", i=PACK),
            )

        make_h(0)
        make_h(1)
        for a in range(K_PASSES):
            weave_w1_pair(a, 1)
        change_page(0, slice(0, BANK))
        change_page(0, slice(BANK, S))
        for a in range(K_PASSES):
            quant_w1_pair(a, 1)
        row_top(0)
        make_h(2)
        make_h(3)
        for a in range(K_PASSES):
            weave_w1(a)
        change_page(1)
        row_top(1)
        look_first = ring.tile([P, PACK, M], F32, name="look_first", tag="raw_last")
        look(0, look_first[:, 0, :])
        look(1, look_first[:, 1, :])
        change_page(2)
        change_page(3)
        planes_second = ring.tile([P, K_PASSES, PASS], U8, name="planes_second", tag="h2", align_bytes=64)
        for a in range(K_PASSES):
            quant_w1(a, planes_second[:, a, :])
        x_nat = [ring.tile([P, 2, M], BF16, name="x_nat0", tag="bf_own1", align_bytes=64)]
        nc.gpsimd.tensor_tensor(out=x_nat[0][:], in0=look_first[:, 0:2, :], in1=fam_sb[0][:, 0:2, :], op=ALU.mult)
        make_h(4)
        make_h(5)
        mid_tops = ring.tile([P, 2], F32, name="mid_tops", tag="bf_own2", align_bytes=64)
        neg_top[2], neg_top[3] = mid_tops[:, 0:1], mid_tops[:, 1:2]
        row_top(2)
        row_top(3)
        make_h(7)
        make_h(6)
        look(2, look_first[:, 2, :])
        look(3, look_first[:, 3, :])
        weave_w3(0)
        change_page(4)
        change_page(5)
        x_nat.append(ring.tile([P, 2, M], BF16, name="x_nat1", tag="h1", align_bytes=64))
        nc.gpsimd.tensor_tensor(out=x_nat[1][:], in0=look_first[:, 2:4, :], in1=fam_sb[0][:, 2:4, :], op=ALU.mult)
        row_top(4)
        row_top(5)
        look(4, look_mid[:, 0, :])
        look(5, look_mid[:, 1, :])
        weave_w3(1)
        w3_plane = [keep.tile([P, N], U8, name="w3s%d" % b, align_bytes=64) for b in range(R_PASSES)]
        x_plane = [keep.tile([P, M], U8, name="xs%d" % b, align_bytes=64) for b in range(R_PASSES)]
        x_rows = ring.tile([P, PACK, M], BF16, name="x_rows", tag="wgs1", align_bytes=64)
        for i in range(PACK):
            for j in range(PACK):
                nc.sync.dma_start(out=x_rows[i * QUAD : (i + 1) * QUAD, j, :], in_=x_nat[i // 2][j:P:PACK, i % 2, :])
        nc.scalar.copy(
            out=x_bf[0][:].rearrange("p (c i) t -> p c t i", i=PACK),
            in_=x_rows[:].rearrange("p t (c i) -> p c t i", i=PACK),
        )
        change_page(6)
        change_page(7)
        x_mid = ring.tile([P, 2, M], BF16, name="x_mid", tag="wgs2", align_bytes=64)
        nc.vector.tensor_tensor(out=x_mid[:], in0=look_mid[:], in1=fam_sb[1][:, 0:2, :], op=ALU.mult)
        x_bf.append(ring.tile([P, M, PACK], BF16, name="x_bf1", tag="h1", align_bytes=64))
        nc.scalar.copy(out=x_bf[1][:, :, 0:2], in_=x_mid[:].rearrange("p t m -> p m t"))
        last_tops = ring.tile([P, 2], F32, name="last_tops", tag="wgs1", align_bytes=64)
        neg_top[6], neg_top[7] = last_tops[:, 0:1], last_tops[:, 1:2]
        x_first = ring.tile([P, M], U32, name="x_first", tag="wgs3", align_bytes=64)
        row_top(6)
        quantize(x_first[:], x_plane[0][:], x_bf[0][:])
        row_top(7)
        look_last = keep.tile([P, 2, M], F32, name="look_last")
        look(6, look_last[:, 0, :])
        look(7, look_last[:, 1, :])
        x_last = keep.tile([P, M], U32, name="x_last", align_bytes=64)
        x_codes = [x_first[:], x_last[:]]
        w3_both = ring.tile([P, R_PASSES, N], U32, name="w3_both", tag="x_bf0", align_bytes=64)
        w3_codes = [w3_both[:, b, :] for b in range(R_PASSES)]
        for b in range(R_PASSES):
            quantize(w3_codes[b], w3_plane[b][:], w3_bf[b][:])
        nc.vector.tensor_tensor(
            out=x_bf[1][:, :, 2:4],
            in0=look_last[:].rearrange("p t m -> p m t"),
            in1=fam_sb[1][:, 2:4, :].rearrange("p t m -> p m t"),
            op=ALU.mult,
        )
        quantize(x_codes[1], x_plane[1][:], x_bf[1][:])

        y_acc = [psum.tile([P, BANK], F32, name="y%d" % c, tag="bank%d" % (2 * c)) for c in range(N // P)]
        d_acc = [psum.tile([P, BANK], F32, name="d%d" % c, tag="bank%d" % (2 * c + 1)) for c in range(N // P)]

        def y_pass(b, c):
            nc.tensor.matmul_mx(
                out=y_acc[c][:],
                lhsT=w2_codes[:, b, 2 * c * P : 2 * (c + 1) * P].bitcast(FP4X4),
                lhsT_scale=w2_plane[:, b, c * P : (c + 1) * P],
                rhs=x_codes[b].bitcast(FP8X4),
                rhs_scale=x_plane[b][:],
                start=(b == 0),
                stop=(b == R_PASSES - 1),
            )

        def d_pass(b, c):
            nc.tensor.matmul_mx(
                out=d_acc[c][:],
                lhsT=w3_codes[b][:, c * P : (c + 1) * P].bitcast(FP8X4),
                lhsT_scale=w3_plane[b][:, c * P : (c + 1) * P],
                rhs=x_codes[b].bitcast(FP8X4),
                rhs_scale=x_plane[b][:],
                start=(b == 0),
                stop=(b == R_PASSES - 1),
            )

        for c in range(N // P):
            y_pass(0, c)
        for c in range(N // P):
            d_pass(0, c)
        for c in range(N // P):
            y_pass(1, c)
            d_pass(1, c)
        y_sb = ring.tile([P, N // P, M], F32, name="y_sb", tag="raw_last")
        res = ring.tile([P, N // P, M], F32, name="res", tag="wide", bufs=7)
        for c in range(N // P):
            nc.scalar.copy(out=y_sb[:, c, :], in_=y_acc[c][:])
            nc.vector.scalar_tensor_tensor(
                out=res[:, c, :], in0=d_acc[c][:], scalar=base_sb[:, c : c + 1], in1=y_sb[:, c, :], op0=ALU.add, op1=ALU.max
            )
            nc.sync.dma_start(out=out[c * P : (c + 1) * P, :], in_=res[:, c, :])
